import numpy as np
import ml_dtypes


def mxq(x, axis, fmt="e4m3"):
    dtype, down = {"e4m3": (ml_dtypes.float8_e4m3fn, 7), "e5m2": (ml_dtypes.float8_e5m2, 14)}[fmt]
    v = np.moveaxis(np.asarray(x, np.float32).astype(ml_dtypes.bfloat16).astype(np.float64), axis, -1)
    blocks = v.reshape(v.shape[:-1] + (-1, 32))
    amax = np.abs(blocks).max(-1, keepdims=True)
    byte = np.maximum(np.where(amax > 0, np.frexp(amax)[1] - 1 + 127, 0) - down, 1)
    scale = np.exp2(byte - 127.0)
    codes = (blocks / scale).astype(np.float32).astype(dtype).astype(np.float64)
    return np.moveaxis((codes * scale).reshape(v.shape), -1, axis)


WIDE = False


def mx_kscale(k):
    if not WIDE:
        return np.ones(k)
    levels = np.array([10, -10, 5, -5, 0])
    if k % 512:
        return np.exp2(np.random.permutation(np.resize(levels, k // 32))).repeat(32)
    a = np.empty((k // 512, 16))
    for p in range(k // 512):
        a[p, :8] = np.random.permutation(np.resize(levels, 8))
        for g in range(8):
            far = levels[np.abs(levels - a[p, g]) >= 10]
            a[p, g + 8] = far[np.random.randint(len(far))]
    return np.exp2(a.ravel()).repeat(32)


def f64(x):
    return np.asarray(x).astype(np.float64)


def striped(idx):
    return np.tile(idx.reshape(-1, 16).T, (8, 1)).astype(np.uint16)


def unstriped(offs):
    return offs[:16].T.reshape(-1).astype(np.int64)


E2M1 = np.array([0.0, 0.5, 1.0, 1.5, 2.0, 3.0, 4.0, 6.0, -0.0, -0.5, -1.0, -1.5, -2.0, -3.0, -4.0, -6.0])


def pack_weight(w, fmt):
    k, n = w.shape
    w = f64(np.asarray(w, np.float32).astype(ml_dtypes.bfloat16)).reshape(k // 32, 32, n)
    amax = np.abs(w).max(1)
    if fmt == "e4m3":
        byte = np.frexp(amax)[1] - 1 + 127 - 7
    else:
        mant, ex = np.frexp(amax / 6.0)
        byte = np.where(mant > 0.5, ex, ex - 1) + 127
    byte = np.clip(np.where(amax > 0, byte, 1), 1, 254)
    scaled = (w * np.exp2(127.0 - byte)[:, None, :]).reshape(k, n).astype(np.float32)
    by_word = np.ascontiguousarray(scaled.reshape(k // 512, 128, 4, n).transpose(0, 1, 3, 2))
    if fmt == "e4m3":
        words = by_word.astype(ml_dtypes.float8_e4m3fn).view(np.uint8)
    else:
        c = by_word.astype(ml_dtypes.float4_e2m1fn).view(np.uint8) & 0xF
        words = (c[..., 0::2] | (c[..., 1::2] << 4)).reshape(k // 512, 128, 2 * n)
    return np.ascontiguousarray(words), np.ascontiguousarray(byte.astype(np.uint8).reshape(k // 512, 16, n))


def unpack_weight(words, scales, fmt):
    g, _, n = scales.shape
    words = np.ascontiguousarray(words).reshape(g, 128, n, -1)
    if fmt == "e4m3":
        vals = words.view(ml_dtypes.float8_e4m3fn).astype(np.float64)
    else:
        nib = np.empty((g, 128, n, 4), np.uint8)
        nib[..., 0::2] = words & 0xF
        nib[..., 1::2] = words >> 4
        vals = E2M1[nib]
    vals = vals * np.repeat(np.exp2(scales.astype(np.float64) - 127.0), 8, axis=1)[..., None]
    return vals.transpose(0, 1, 3, 2).reshape(g * 512, n)


def gelu(v):
    return 0.5 * v * (1.0 + np.tanh(np.sqrt(2.0 / np.pi) * (v + 0.044715 * v**3)))


def bf(x):
    return np.asarray(x, np.float32).astype(ml_dtypes.bfloat16)


def planes(Y):
    n, m = Y.shape
    b = f64(bf(Y)).reshape(n // 32, 32, m)
    amax = np.abs(b).max(1)
    byte = np.clip(np.where(amax > 0, np.frexp(amax)[1] - 1 + 127 - 7, 1), 1, 254)
    codes = (b * np.exp2(127.0 - byte)[:, None, :]).reshape(n, m).astype(np.float32).astype(ml_dtypes.float8_e4m3fn).view(np.uint8)
    words = codes.reshape(n // 512, 128, 4, m).transpose(0, 1, 3, 2)
    return np.ascontiguousarray(words), np.ascontiguousarray(byte.astype(np.uint8).reshape(n // 512, 16, m))


K, H, N, T, S, T2 = 1024, 512, 512, 2048, 1024, 2048

def setup_inputs():
    n = np.random.standard_normal
    s, u, w = mx_kscale(K)[:, None], mx_kscale(H)[:, None], mx_kscale(S)[:, None]
    tab_words, tab_scales = pack_weight(n((K, T)) * s, "e4m3")
    wl_words, wl_scales = pack_weight(n((K, H)) / np.sqrt(K) / s * u.T, "e2m1")
    wo_words, wo_scales = pack_weight(n((H, N)) * np.exp(0.8 * n((1, N))) / np.sqrt(H) / u, "e4m3")
    return {
        "tab_words": tab_words, "tab_scales": tab_scales,
        "offs": striped(np.random.permutation(T)[:S]),
        "offs2": striped(np.random.permutation(T2)[:S]),
        "offs3": striped(np.random.permutation(T2)[:S]),
        "wl_words": wl_words, "wl_scales": wl_scales,
        "wr": (n((K, H)) / np.sqrt(K) / s * u.T).astype(np.float32),
        "note": (np.exp(0.3 * n(S)) * w[:, 0]).astype(np.float32),
        "mix": (n((S, S)) / np.sqrt(S) / w).astype(np.float32),
        "wg1": np.exp(0.3 * n((128, S))).astype(np.float32),
        "wg2": np.exp(0.3 * n((128, S))).astype(np.float32),
        "tempo": (n((H, T2)) * u).astype(np.float32),
        "wo_words": wo_words, "wo_scales": wo_scales,
    }

def reference(tab_words, tab_scales, offs, offs2, offs3, wl_words, wl_scales, wr, note, mix,
              wg1, wg2, tempo, wo_words, wo_scales):
    v = unpack_weight(tab_words, tab_scales, "e4m3")[:, unstriped(offs)]
    h1 = unpack_weight(wl_words, wl_scales, "e2m1").T @ v
    b = (v.T @ mxq(f64(wr), 0, "e4m3")) * f64(note)[:, None]
    h2 = mxq(b, 0, "e4m3").T @ mxq(f64(mix), 0, "e4m3")
    pageA = np.zeros((H, T2))
    pageA[:, unstriped(offs2)] = np.tile(f64(wg1), (H // 128, 1)) * h1
    pageB = np.zeros((H, T2))
    pageB[:, unstriped(offs3)] = np.tile(f64(wg2), (H // 128, 1)) * h2
    z = np.abs(pageA + f64(tempo)) - np.abs(pageB)
    y = unpack_weight(wo_words, wo_scales, "e4m3").T @ mxq(z, 0, "e4m3")
    words, scales = planes(y)
    return y, words, scales

@@ -1,0 +1,343 @@
+from contextlib import ExitStack
+
+import concourse.mybir as mybir
+from concourse.masks import make_identity
+
+K, H, N, T, S, T2 = 1024, 512, 512, 2048, 1024, 2048
+FLOPS = 2 * (K * H * S + S * K * H + S * H * S + H * N * T2)
+
+F32 = mybir.dt.float32
+BF16 = mybir.dt.bfloat16
+I32 = mybir.dt.int32
+U32 = mybir.dt.uint32
+U16 = mybir.dt.uint16
+U8 = mybir.dt.uint8
+FP8X4 = mybir.dt.float8_e4m3fn_x4
+FP4X4 = mybir.dt.float4_e2m1fn_x4
+MULT = mybir.AluOpType.mult
+SUBTRACT = mybir.AluOpType.subtract
+COPY = mybir.ActivationFunctionType.Copy
+ABS = mybir.ActivationFunctionType.Abs
+
+P = 128
+HALF = 512
+LIST_COLS = HALF // 16
+CHUNK = 256
+CHUNKS = T2 // CHUNK
+WIDE = 512
+
+
+def tile_list_two_hand_loads_kernel(
+    tc, tab_words, tab_scales, offs, offs2, offs3, wl_words, wl_scales, wr, note, mix,
+    wg1, wg2, tempo, wo_words, wo_scales, out_0, out_1, out_2,
+):
+    nc = tc.nc
+    with ExitStack() as ctx:
+        lists = ctx.enter_context(tc.tile_pool(name="lists", bufs=1))
+        sb = ctx.enter_context(tc.tile_pool(name="sb", bufs=1))
+        psum = ctx.enter_context(tc.psum_pool(name="psum", bufs=1))
+
+        def new(name, shape, dtype, slot=None, bufs=1):
+            return sb.tile(shape, dtype, name=name, tag=slot or name, bufs=bufs, align_bytes=64)
+
+        def bank(name, kind):
+            return psum.tile([P, 512], F32, name=name, tag=kind, bufs={"left": 1, "acc": 3, "turn": 4}[kind])
+
+        def load_scale_rows(tile, src, passes):
+            for q in range(4):
+                nc.sync.dma_start(
+                    tile[32 * q : 32 * q + 4, :].bitcast(I32).rearrange("p (a c) -> p a c", a=passes),
+                    src[:, 4 * q : 4 * q + 4, :].rearrange("a r c -> r a c").bitcast(I32),
+                )
+
+        def weave(engine_copy, dst, src, run):
+            engine_copy(
+                dst.rearrange("p (c e i) -> p c i e", e=run, i=4),
+                src.rearrange("p i (c e) -> p c i e", e=run),
+            )
+
+        def quantize(codes, scales, values):
+            nc.vector.quantize_mx(out=codes.bitcast(FP8X4), scales=scales, in_=values)
+
+        def clear_page(page):
+            for c in range(0, T2, 512):
+                nc.gpsimd.memset(page[:, c : c + 512], 0.0)
+
+        tab_s = new("tab_s", [P, T], U8)
+        v_s1 = new("v_s1", [P, S], U8)
+        wl_s = new("wl_s", [P, 2 * H], U8)
+        wo_s_raw = new("wo_s_raw", [P, N], U8)
+        nc.gpsimd.memset(tab_s[:].bitcast(I32), 0)
+        nc.gpsimd.memset(wl_s[:].bitcast(I32), 0)
+        nc.gpsimd.memset(v_s1[:].bitcast(I32), 0)
+        page_a = [new("page_a0", [P, T2], F32), new("page_a1", [P, T2], F32)]
+        nc.vector.memset(page_a[0][:], 0.0)
+        nc.vector.memset(page_a[1][:], 0.0)
+        nc.gpsimd.memset(wo_s_raw[:].bitcast(I32), 0)
+        ident = new("ident", [P, P], F32)
+        make_identity(nc, ident[:])
+        note_rows = new("note_rows", [P, P], F32)
+        nc.gpsimd.memset(note_rows[:], 0.0)
+
+        idx = lists.tile([P, S // 16], U16, name="idx")
+        idx2 = lists.tile([P, S // 16], U16, name="idx2")
+        idx3 = lists.tile([P, S // 16], U16, name="idx3")
+        tab_w = [new(f"tab_w{a}", [P, T], I32) for a in range(2)]
+        nc.sync.dma_start(idx[:], offs)
+        for q in range(4):
+            nc.sync.dma_start(tab_s[32 * q : 32 * q + 8, :].bitcast(I32), tab_scales[:, 4 * q : 4 * q + 4, :].bitcast(I32))
+        for a in range(2):
+            nc.sync.dma_start(tab_w[a][:], tab_words[a].rearrange("p t i -> p (t i)").bitcast(I32))
+        wl_w = new("wl_w", [P, 2, 2 * H], U8)
+        nc.sync.dma_start(wl_w[:].bitcast(I32), wl_words.rearrange("a p n -> p a n").bitcast(I32))
+        load_scale_rows(wl_s, wl_scales, 2)
+        nc.sync.dma_start(idx2[:], offs2)
+        wg1_t = new("wg1_t", [P, S], F32)
+        nc.sync.dma_start(wg1_t[:], wg1)
+        wr_raw = [new(f"wr_raw{a}", [P, 4, H], F32) for a in range(2)]
+        for a in range(2):
+            nc.sync.dma_start(wr_raw[a][:], wr[512 * a : 512 * (a + 1), :].rearrange("(p i) r -> p i r", i=4))
+        for a in range(2):
+            nc.sync.dma_start(
+                note_rows[4 * a : 4 * a + 4, :].rearrange("i (g q) -> i g q", q=8),
+                note[512 * a : 512 * (a + 1)].rearrange("(g i q) -> i g q", i=4, q=8),
+            )
+        note_turned = bank("note_turned", "turn")
+        nc.tensor.transpose(note_turned[:, 0:P], note_rows[:], ident[:])
+        note_t = new("note_t", [P, 8], F32)
+        nc.scalar.copy(note_t[:], note_turned[:, 0:8])
+        mix_raw = {}
+        for h in range(2):
+            for a in range(2):
+                mix_raw[a, h] = new(f"mix_raw{a}{h}", [P, 4, HALF], F32)
+                rows = mix[512 * a : 512 * (a + 1), HALF * h : HALF * (h + 1)].rearrange("(g i q) j -> i g q j", i=4, q=8)
+                for i in range(4):
+                    nc.sync.dma_start(mix_raw[a, h][:, i, :], rows[i])
+        nc.sync.dma_start(idx3[:], offs3)
+        wo_w_raw = new("wo_w_raw", [P, N], I32)
+        nc.sync.dma_start(wo_w_raw[:], wo_words[0].rearrange("p c i -> p (c i)").bitcast(I32))
+        load_scale_rows(wo_s_raw, wo_scales, 1)
+        wg2_t = new("wg2_t", [P, 4, S], F32)
+        for k in range(4):
+            nc.sync.dma_start(wg2_t[32 * k : 32 * (k + 1), :, :], wg2.rearrange("(q i) j -> q i j", i=4))
+
+        v_w = [new(f"v_w{a}", [P, S], U32) for a in range(2)]
+        v_s_raw = new("v_s_raw", [P, S], U8)
+        v_s0 = new("v_s0", [P, S], U8)
+        v_s = [v_s0, v_s1]
+
+        def gather_words(a, h):
+            nc.vector.tensor_copy(
+                v_w[a][:, HALF * h : HALF * (h + 1)].rearrange("p (i g q) -> p g i q", i=4, q=8),
+                tab_w[a][:].bitcast(U32).indirect(idx[:, LIST_COLS * h : LIST_COLS * (h + 1)]),
+            )
+
+        nc.vector.tensor_copy(v_s_raw[:], tab_s[:].indirect(idx[:]))
+        nc.vector.tensor_copy(
+            v_s0[:].bitcast(I32).rearrange("p (b i g w) -> p b g i w", i=4, g=16, w=2),
+            v_s_raw[:].bitcast(I32).rearrange("p (b g i w) -> p b g i w", i=4, g=16, w=2),
+        )
+        for q in range(4):
+            nc.scalar.dma_start(v_s1[32 * q : 32 * q + 4, :].bitcast(I32), v_s0[32 * q + 4 : 32 * q + 8, :].bitcast(I32))
+        for a in range(2):
+            gather_words(a, 0)
+            gather_words(a, 1)
+
+        page_a.extend(new(f"page_a{2 + a}", [P, T2], F32, slot=f"tab_w{a}") for a in range(2))
+        clear_page(page_a[2])
+        clear_page(page_a[3])
+
+        def left_hand(s, h, slot):
+            acc = bank("left_acc", "left")
+            for a in range(2):
+                nc.tensor.matmul_mx(
+                    out=acc[:],
+                    lhsT=wl_w[:, a, 2 * P * s : 2 * P * (s + 1)].bitcast(FP4X4),
+                    lhsT_scale=wl_s[:, H * a + P * s : H * a + P * (s + 1)],
+                    rhs=v_w[a][:, HALF * h : HALF * (h + 1)].bitcast(FP8X4),
+                    rhs_scale=v_s[a][:, HALF * h : HALF * (h + 1)],
+                    start=(a == 0), stop=(a == 1),
+                )
+            h1 = new(f"h1_{s}{h}", [P, HALF], F32, slot=slot)
+            nc.scalar.copy(
+                h1[:].rearrange("p (g i q) -> p g i q", i=4, q=8),
+                acc[:].rearrange("p (i g q) -> p g i q", i=4, q=8),
+            )
+            nc.vector.tensor_tensor(
+                page_a[s][:].indirect(idx2[:, LIST_COLS * h : LIST_COLS * (h + 1)]),
+                h1[:], wg1_t[:, HALF * h : HALF * (h + 1)], MULT,
+            )
+
+        wr_w = new("wr_w", [P, 2 * H], U32)
+        wr_s = new("wr_s", [P, 2 * H], U8)
+        mix_w = new("mix_w", [P, 2 * S], U32)
+        mix_s = new("mix_s", [P, 2 * S], U8)
+        b_w = new("b_w", [P, 2 * H], U32)
+        b_s = new("b_s", [P, 2 * H], U8)
+
+        def quantize_wr(a):
+            woven = new(f"wr_bf{a}", [P, 4 * H], BF16)
+            weave(nc.scalar.copy, woven[:], wr_raw[a][:], 2)
+            quantize(wr_w[:, H * a : H * (a + 1)], wr_s[:, H * a : H * (a + 1)], woven[:])
+
+        def quantize_mix(a, h):
+            woven = new(f"mix_bf{a}{h}", [P, 4 * HALF], BF16)
+            weave(nc.scalar.copy, woven[:], mix_raw[a, h][:], 2)
+            cols = slice(S * a + HALF * h, S * a + HALF * (h + 1))
+            quantize(mix_w[:, cols], mix_s[:, cols], woven[:])
+
+        def make_b(blk):
+            rows = new(f"b_rows{blk}", [P, 4, H], BF16)
+            for i in range(4):
+                acc = bank("b_acc", "acc")
+                first = HALF * blk + P * i
+                for a in range(2):
+                    nc.tensor.matmul_mx(
+                        out=acc[:],
+                        lhsT=v_w[a][:, first : first + P].bitcast(FP8X4),
+                        lhsT_scale=v_s[a][:, first : first + P],
+                        rhs=wr_w[:, H * a : H * (a + 1)].bitcast(FP8X4),
+                        rhs_scale=wr_s[:, H * a : H * (a + 1)],
+                        start=(a == 0), stop=(a == 1),
+                    )
+                nc.scalar.activation(
+                    rows[:, i, :].rearrange("p (u m) -> p u m", u=4),
+                    acc[:].rearrange("p (m u) -> p u m", u=4),
+                    COPY, scale=note_t[:, 4 * blk + i : 4 * blk + i + 1],
+                )
+            woven = new(f"b_bf{blk}", [P, 4 * H], BF16)
+            weave(nc.scalar.copy, woven[:], rows[:], 4)
+            quantize(b_w[:, H * blk : H * (blk + 1)], b_s[:, H * blk : H * (blk + 1)], woven[:])
+
+        left_hand(0, 0, "h2_2")
+        left_hand(1, 0, "h2_3")
+        quantize_wr(0)
+        quantize_wr(1)
+        left_hand(0, 1, "wr_raw1")
+        quantize_mix(0, 0)
+        left_hand(1, 1, "mix_raw00")
+        make_b(0)
+        left_hand(2, 0, "b_rows0")
+        quantize_mix(1, 0)
+        left_hand(3, 0, "mix_raw10")
+        make_b(1)
+        left_hand(2, 1, "b_rows1")
+        quantize_mix(0, 1)
+        quantize_mix(1, 1)
+        left_hand(3, 1, "mix_raw11")
+
+        page_b_slots = ["wr_raw0", "wr_raw1", "tab_s", "v_s_raw"]
+        page_b = [new(f"page_b{i}", [P, T2], F32, slot=page_b_slots[i]) for i in range(4)]
+        for page in page_b:
+            clear_page(page)
+
+        wo_w = new("wo_w", [P, N], I32)
+        wo_s = new("wo_s", [P, N], U8)
+        nc.vector.tensor_copy(wo_w[:].rearrange("p (i m) -> p i m", i=4), wo_w_raw[:].rearrange("p (m i) -> p i m", i=4))
+        nc.vector.tensor_copy(wo_s[:].rearrange("p (i m) -> p i m", i=4), wo_s_raw[:].rearrange("p (m i) -> p i m", i=4))
+
+        h2 = [new(f"h2_{i}", [P, S], F32, slot=(f"v_w{i}" if i < 2 else f"h2_{i}")) for i in range(4)]
+        for h in range(2):
+            for i in range(4):
+                acc = bank("h2_acc", "acc")
+                for a in range(2):
+                    cols = slice(S * a + HALF * h, S * a + HALF * (h + 1))
+                    nc.tensor.matmul_mx(
+                        out=acc[:],
+                        lhsT=b_w[:, H * a + P * i : H * a + P * (i + 1)].bitcast(FP8X4),
+                        lhsT_scale=b_s[:, H * a + P * i : H * a + P * (i + 1)],
+                        rhs=mix_w[:, cols].bitcast(FP8X4),
+                        rhs_scale=mix_s[:, cols],
+                        start=(a == 0), stop=(a == 1),
+                    )
+                nc.scalar.copy(h2[i][:, HALF * h : HALF * (h + 1)], acc[:])
+
+        wide_slots = ["mix_raw00", "mix_raw10", "mix_raw01", "mix_raw11"]
+        staging = ["wr_bf1", "mix_bf00", "b_bf0", "wr_bf0", "b_rows0", "b_rows1", "b_bf1", "mix_bf10"]
+        left_t = [new(f"left_t{c}", [P, 2, H], F32, slot=staging[c]) for c in range(CHUNKS)]
+        for w in range(T2 // WIDE):
+            tempo_t = new(f"tempo_t{w}", [P, 4, WIDE], F32, slot=wide_slots[w])
+            nc.sync.dma_start(tempo_t[:], tempo[:, WIDE * w : WIDE * (w + 1)].rearrange("(s p) t -> p s t", p=P))
+            for j in range(WIDE // P):
+                beat = WIDE * w + P * j
+                turned = bank("turned", "turn")
+                for s in range(4):
+                    nc.tensor.matmul(turned[:, P * s : P * (s + 1)], page_a[s][:, beat : beat + P], ident[:],
+                                     start=True, stop=False, is_transpose=True)
+                    nc.tensor.matmul(turned[:, P * s : P * (s + 1)], tempo_t[:, s, P * j : P * (j + 1)], ident[:],
+                                     start=False, stop=True, is_transpose=True)
+                nc.scalar.activation(
+                    left_t[beat // CHUNK][:, (beat % CHUNK) // P, :].rearrange("p (i m) -> p i m", i=4),
+                    turned[:].rearrange("p (m i) -> p i m", i=4),
+                    ABS,
+                )
+
+        page_a_slots = ["page_a0", "page_a1", "tab_w0", "tab_w1"]
+        right = [new(f"right{w}", [P, 4, WIDE], F32, slot=page_a_slots[w]) for w in range(T2 // WIDE)]
+        for i in range(4):
+            page = page_b[i]
+            nc.vector.tensor_tensor(page[:].indirect(idx3[:]), h2[i][:], wg2_t[:, i, :], MULT)
+            width = WIDE if i < 3 else CHUNK
+            for c in range(0, T2, width):
+                nc.scalar.activation(right[c // WIDE][:, i, c % WIDE : c % WIDE + width], page[:, c : c + width], ABS)
+
+        y_w = new("y_w", [P, T2], I32)
+        y_s = new("y_s", [P, T2], U8)
+        out_rows = out_0.rearrange("(p i) t -> p i t", i=4)
+        out_words = out_1[0].rearrange("p m i -> p (m i)").bitcast(I32)
+        z_bf, z_w, z_s, y_f, y_bf = {}, {}, {}, {}, {}
+
+        def make_z(c):
+            z_bf[c] = new("z_bf", [P, 4 * CHUNK], BF16, bufs=2)
+            for j in range(CHUNK // P):
+                back = bank("back", "turn")
+                for i in range(4):
+                    nc.tensor.transpose(back[:, P * i : P * (i + 1)], left_t[c][:, j, P * i : P * (i + 1)], ident[:])
+                beat = CHUNK * c + P * j
+                nc.vector.tensor_tensor(
+                    z_bf[c][:, 4 * P * j : 4 * P * (j + 1)].rearrange("p (c e i) -> p c i e", e=2, i=4),
+                    back[:].rearrange("p (i c e) -> p c i e", e=2, i=4),
+                    right[beat // WIDE][:, :, beat % WIDE : beat % WIDE + P].rearrange("p i (c e) -> p c i e", e=2),
+                    SUBTRACT,
+                )
+
+        def make_y(c):
+            z_w[c] = new("z_w", [P, CHUNK], U32, bufs=2)
+            z_s[c] = new("z_s", [P, CHUNK], U8, bufs=2)
+            quantize(z_w[c][:], z_s[c][:], z_bf[c][:])
+            y_f[c] = new(f"y_f{c}", [P, 4, CHUNK], F32, slot=wide_slots[c % 4])
+            for pair in range(2):
+                acc = bank("y_acc", "acc")
+                for u in range(2):
+                    i = 2 * pair + u
+                    nc.tensor.matmul_mx(
+                        out=acc[:, CHUNK * u : CHUNK * (u + 1)],
+                        lhsT=wo_w[:, P * i : P * (i + 1)].bitcast(FP8X4),
+                        lhsT_scale=wo_s[:, P * i : P * (i + 1)],
+                        rhs=z_w[c][:].bitcast(FP8X4),
+                        rhs_scale=z_s[c][:],
+                        start=True, stop=True,
+                    )
+                nc.scalar.copy(y_f[c][:, 2 * pair : 2 * pair + 2, :], acc[:].rearrange("p (u t) -> p u t", u=2))
+            nc.sync.dma_start(out_rows[:, :, CHUNK * c : CHUNK * (c + 1)], y_f[c][:])
+
+        def round_y(c):
+            y_bf[c] = new("y_bf", [P, 4 * CHUNK], BF16, bufs=2)
+            weave(nc.vector.tensor_copy if c % 2 == 1 else nc.scalar.copy, y_bf[c][:], y_f[c][:], 2)
+
+        def planes_y(c):
+            cols = slice(CHUNK * c, CHUNK * (c + 1))
+            quantize(y_w[:, cols], y_s[:, cols], y_bf[c][:])
+            nc.sync.dma_start(out_words[:, cols], y_w[:, cols])
+
+        make_z(0)
+        make_y(0)
+        for c in range(CHUNKS):
+            if c + 1 < CHUNKS:
+                make_z(c + 1)
+            round_y(c)
+            if c + 1 < CHUNKS:
+                make_y(c + 1)
+            planes_y(c)
+        for q in range(4):
+            nc.sync.dma_start(out_2[0, 4 * q : 4 * q + 4, :].bitcast(I32), y_s[32 * q : 32 * q + 4, :].bitcast(I32))

@@ -20,6 +20,8 @@ COPY = mybir.ActivationFunctionType.Copy
 ABS = mybir.ActivationFunctionType.Abs
 
 P = 128
+KB = 1024
+BANK = 2048
 HALF = 512
 LIST_COLS = HALF // 16
 CHUNK = 256
@@ -37,15 +39,15 @@ def tile_list_two_hand_loads_kernel(
         sb = ctx.enter_context(tc.tile_pool(name="sb", bufs=1))
         psum = ctx.enter_context(tc.psum_pool(name="psum", bufs=1))
 
-        def new(name, shape, dtype, slot=None, bufs=1):
-            return sb.tile(shape, dtype, name=name, tag=slot or name, bufs=bufs, align_bytes=64)
+        def new(name, shape, dtype, kb):
+            return sb.tile(shape, dtype, name=name, tag=name, align_bytes=64, offset=int(kb * KB))
 
-        def bank(name, kind):
-            return psum.tile([P, 512], F32, name=name, tag=kind, bufs={"left": 1, "acc": 3, "turn": 4}[kind])
+        def bank(name, number):
+            return psum.tile([P, 512], F32, name=name, tag=name, offset=number * BANK)
 
-        def load_scale_rows(tile, src, passes):
+        def load_scale_rows(queue, tile, src, passes):
             for q in range(4):
-                nc.sync.dma_start(
+                queue.dma_start(
                     tile[32 * q : 32 * q + 4, :].bitcast(I32).rearrange("p (a c) -> p a c", a=passes),
                     src[:, 4 * q : 4 * q + 4, :].rearrange("a r c -> r a c").bitcast(I32),
                 )
@@ -63,67 +65,38 @@ def tile_list_two_hand_loads_kernel(
             for c in range(0, T2, 512):
                 nc.gpsimd.memset(page[:, c : c + 512], 0.0)
 
-        tab_s = new("tab_s", [P, T], U8)
-        v_s1 = new("v_s1", [P, S], U8)
-        wl_s = new("wl_s", [P, 2 * H], U8)
-        wo_s_raw = new("wo_s_raw", [P, N], U8)
-        nc.gpsimd.memset(tab_s[:].bitcast(I32), 0)
+        tab_s = new("tab_s", [P, T], U8, 172)
+        wl_s = new("wl_s", [P, 2 * H], U8, 178)
+        v_s1 = new("v_s1", [P, S], U8, 175)
+        nc.vector.memset(tab_s[32:64, :].bitcast(I32), 0)
+        nc.vector.memset(tab_s[64:128, :].bitcast(I32), 0)
+        nc.vector.memset(v_s1[:].bitcast(I32), 0)
         nc.gpsimd.memset(wl_s[:].bitcast(I32), 0)
-        nc.gpsimd.memset(v_s1[:].bitcast(I32), 0)
-        page_a = [new("page_a0", [P, T2], F32), new("page_a1", [P, T2], F32)]
-        nc.vector.memset(page_a[0][:], 0.0)
-        nc.vector.memset(page_a[1][:], 0.0)
-        nc.gpsimd.memset(wo_s_raw[:].bitcast(I32), 0)
-        ident = new("ident", [P, P], F32)
+        page_a = [new(f"page_a{s}", [P, T2], F32, 16 + 8 * s) for s in range(4)]
+        clear_page(page_a[0])
+        clear_page(page_a[1])
+        ident = new("ident", [P, P], F32, 181.5)
         make_identity(nc, ident[:])
-        note_rows = new("note_rows", [P, P], F32)
+        note_rows = new("note_rows", [P, P], F32, 182)
         nc.gpsimd.memset(note_rows[:], 0.0)
+        clear_page(page_a[2])
+        clear_page(page_a[3])
 
         idx = lists.tile([P, S // 16], U16, name="idx")
         idx2 = lists.tile([P, S // 16], U16, name="idx2")
         idx3 = lists.tile([P, S // 16], U16, name="idx3")
-        tab_w = [new(f"tab_w{a}", [P, T], I32) for a in range(2)]
+        tab_w = [new(f"tab_w{a}", [P, T], I32, 8 * a) for a in range(2)]
         nc.sync.dma_start(idx[:], offs)
-        for q in range(4):
-            nc.sync.dma_start(tab_s[32 * q : 32 * q + 8, :].bitcast(I32), tab_scales[:, 4 * q : 4 * q + 4, :].bitcast(I32))
+        nc.sync.dma_start(tab_s[0:32, :].bitcast(I32), tab_scales.rearrange("a r t -> (a r) t").bitcast(I32))
+        load_scale_rows(nc.sync, wl_s, wl_scales, 2)
+        wl_w = new("wl_w", [P, 2, 2 * H], U8, 176)
+        nc.sync.dma_start(wl_w[:].bitcast(I32), wl_words.rearrange("a p n -> p a n").bitcast(I32))
         for a in range(2):
             nc.sync.dma_start(tab_w[a][:], tab_words[a].rearrange("p t i -> p (t i)").bitcast(I32))
-        wl_w = new("wl_w", [P, 2, 2 * H], U8)
-        nc.sync.dma_start(wl_w[:].bitcast(I32), wl_words.rearrange("a p n -> p a n").bitcast(I32))
-        load_scale_rows(wl_s, wl_scales, 2)
-        nc.sync.dma_start(idx2[:], offs2)
-        wg1_t = new("wg1_t", [P, S], F32)
-        nc.sync.dma_start(wg1_t[:], wg1)
-        wr_raw = [new(f"wr_raw{a}", [P, 4, H], F32) for a in range(2)]
-        for a in range(2):
-            nc.sync.dma_start(wr_raw[a][:], wr[512 * a : 512 * (a + 1), :].rearrange("(p i) r -> p i r", i=4))
-        for a in range(2):
-            nc.sync.dma_start(
-                note_rows[4 * a : 4 * a + 4, :].rearrange("i (g q) -> i g q", q=8),
-                note[512 * a : 512 * (a + 1)].rearrange("(g i q) -> i g q", i=4, q=8),
-            )
-        note_turned = bank("note_turned", "turn")
-        nc.tensor.transpose(note_turned[:, 0:P], note_rows[:], ident[:])
-        note_t = new("note_t", [P, 8], F32)
-        nc.scalar.copy(note_t[:], note_turned[:, 0:8])
-        mix_raw = {}
-        for h in range(2):
-            for a in range(2):
-                mix_raw[a, h] = new(f"mix_raw{a}{h}", [P, 4, HALF], F32)
-                rows = mix[512 * a : 512 * (a + 1), HALF * h : HALF * (h + 1)].rearrange("(g i q) j -> i g q j", i=4, q=8)
-                for i in range(4):
-                    nc.sync.dma_start(mix_raw[a, h][:, i, :], rows[i])
-        nc.sync.dma_start(idx3[:], offs3)
-        wo_w_raw = new("wo_w_raw", [P, N], I32)
-        nc.sync.dma_start(wo_w_raw[:], wo_words[0].rearrange("p c i -> p (c i)").bitcast(I32))
-        load_scale_rows(wo_s_raw, wo_scales, 1)
-        wg2_t = new("wg2_t", [P, 4, S], F32)
-        for k in range(4):
-            nc.sync.dma_start(wg2_t[32 * k : 32 * (k + 1), :, :], wg2.rearrange("(q i) j -> q i j", i=4))
 
-        v_w = [new(f"v_w{a}", [P, S], U32) for a in range(2)]
-        v_s_raw = new("v_s_raw", [P, S], U8)
-        v_s0 = new("v_s0", [P, S], U8)
+        v_w = [new(f"v_w{a}", [P, S], U32, 124 + 4 * a) for a in range(2)]
+        v_s_raw = new("v_s_raw", [P, S], U8, 51.5)
+        v_s0 = new("v_s0", [P, S], U8, 174)
         v_s = [v_s0, v_s1]
 
         def gather_words(a, h):
@@ -137,18 +110,47 @@ def tile_list_two_hand_loads_kernel(
             v_s0[:].bitcast(I32).rearrange("p (b i g w) -> p b g i w", i=4, g=16, w=2),
             v_s_raw[:].bitcast(I32).rearrange("p (b g i w) -> p b g i w", i=4, g=16, w=2),
         )
-        for q in range(4):
-            nc.scalar.dma_start(v_s1[32 * q : 32 * q + 4, :].bitcast(I32), v_s0[32 * q + 4 : 32 * q + 8, :].bitcast(I32))
+        for a in range(2):
+            for q in range(1 - a, 4):
+                row = 16 * a + 4 * q
+                nc.sync.dma_start(v_s[a][32 * q : 32 * q + 4, :].bitcast(I32), v_s0[row : row + 4, :].bitcast(I32))
         for a in range(2):
             gather_words(a, 0)
             gather_words(a, 1)
 
-        page_a.extend(new(f"page_a{2 + a}", [P, T2], F32, slot=f"tab_w{a}") for a in range(2))
-        clear_page(page_a[2])
-        clear_page(page_a[3])
+        nc.sync.dma_start(idx2[:], offs2)
+        wg1_t = new("wg1_t", [P, S], F32, 48)
+        wr_raw = new("wr_raw", [P, 8 * H], F32, 52)
+        wr_pass = [wr_raw[:, 4 * H * a : 4 * H * (a + 1)].rearrange("p (i r) -> p i r", i=4) for a in range(2)]
+        nc.sync.dma_start(wg1_t[:, 0:HALF], wg1[:, 0:HALF])
+        for a in range(2):
+            nc.sync.dma_start(
+                note_rows[4 * a : 4 * a + 4, :].rearrange("i (g q) -> i g q", q=8),
+                note[512 * a : 512 * (a + 1)].rearrange("(g i q) -> i g q", i=4, q=8),
+            )
+        for a in range(2):
+            nc.sync.dma_start(wr_pass[a], wr[512 * a : 512 * (a + 1), :].rearrange("(p i) r -> p i r", i=4))
+        nc.sync.dma_start(wg1_t[:, HALF:S], wg1[:, HALF:S])
+        nc.sync.dma_start(idx3[:], offs3)
+        mix_raw = {}
 
-        def left_hand(s, h, slot):
-            acc = bank("left_acc", "left")
+        def load_mix(a, h, kb):
+            mix_raw[a, h] = new(f"mix_raw{a}{h}", [P, 4, HALF], F32, kb)
+            rows = mix[512 * a : 512 * (a + 1), HALF * h : HALF * (h + 1)].rearrange("(g i q) j -> i g q j", i=4, q=8)
+            for i in range(4):
+                nc.sync.dma_start(mix_raw[a, h][:, i, :], rows[i])
+
+        load_mix(0, 0, 0)
+        load_mix(1, 0, 8)
+        tempo_kb = [84, 108, 68, 76]
+        tempo_t = {}
+
+        def load_tempo(w):
+            tempo_t[w] = new(f"tempo_t{w}", [P, 4, WIDE], F32, tempo_kb[w])
+            nc.sync.dma_start(tempo_t[w][:], tempo[:, WIDE * w : WIDE * (w + 1)].rearrange("(s p) t -> p s t", p=P))
+
+        def left_product(s, h, number, dst):
+            acc = bank(f"left_acc{s}{h}", number)
             for a in range(2):
                 nc.tensor.matmul_mx(
                     out=acc[:],
@@ -158,38 +160,41 @@ def tile_list_two_hand_loads_kernel(
                     rhs_scale=v_s[a][:, HALF * h : HALF * (h + 1)],
                     start=(a == 0), stop=(a == 1),
                 )
-            h1 = new(f"h1_{s}{h}", [P, HALF], F32, slot=slot)
             nc.scalar.copy(
-                h1[:].rearrange("p (g i q) -> p g i q", i=4, q=8),
+                dst.rearrange("p (g i q) -> p g i q", i=4, q=8),
                 acc[:].rearrange("p (i g q) -> p g i q", i=4, q=8),
             )
+
+        def left_half(s, h, kb, number):
+            h1 = new(f"h1_{s}{h}", [P, HALF], F32, kb)
+            left_product(s, h, number, h1[:])
             nc.vector.tensor_tensor(
                 page_a[s][:].indirect(idx2[:, LIST_COLS * h : LIST_COLS * (h + 1)]),
                 h1[:], wg1_t[:, HALF * h : HALF * (h + 1)], MULT,
             )
 
-        wr_w = new("wr_w", [P, 2 * H], U32)
-        wr_s = new("wr_s", [P, 2 * H], U8)
-        mix_w = new("mix_w", [P, 2 * S], U32)
-        mix_s = new("mix_s", [P, 2 * S], U8)
-        b_w = new("b_w", [P, 2 * H], U32)
-        b_s = new("b_s", [P, 2 * H], U8)
+        wr_w = new("wr_w", [P, 2 * H], U32, 152)
+        wr_s = new("wr_s", [P, 2 * H], U8, 156)
+        mix_w = new("mix_w", [P, 2 * S], U32, 157)
+        mix_s = new("mix_s", [P, 2 * S], U8, 165)
+        b_w = new("b_w", [P, 2 * H], U32, 167)
+        b_s = new("b_s", [P, 2 * H], U8, 171)
 
         def quantize_wr(a):
-            woven = new(f"wr_bf{a}", [P, 4 * H], BF16)
-            weave(nc.scalar.copy, woven[:], wr_raw[a][:], 2)
+            woven = new(f"wr_bf{a}", [P, 4 * H], BF16, 112 + 4 * a)
+            weave(nc.scalar.copy, woven[:], wr_pass[a], 2)
             quantize(wr_w[:, H * a : H * (a + 1)], wr_s[:, H * a : H * (a + 1)], woven[:])
 
-        def quantize_mix(a, h):
-            woven = new(f"mix_bf{a}{h}", [P, 4 * HALF], BF16)
+        def quantize_mix(a, h, kb):
+            woven = new(f"mix_bf{a}{h}", [P, 4 * HALF], BF16, kb)
             weave(nc.scalar.copy, woven[:], mix_raw[a, h][:], 2)
             cols = slice(S * a + HALF * h, S * a + HALF * (h + 1))
             quantize(mix_w[:, cols], mix_s[:, cols], woven[:])
 
-        def make_b(blk):
-            rows = new(f"b_rows{blk}", [P, 4, H], BF16)
+        def make_b(blk, kb):
+            rows = new(f"b_rows{blk}", [P, 4, H], BF16, 1 + 8 * blk)
             for i in range(4):
-                acc = bank("b_acc", "acc")
+                acc = bank(f"b_acc{blk}{i}", 2 + i)
                 first = HALF * blk + P * i
                 for a in range(2):
                     nc.tensor.matmul_mx(
@@ -205,66 +210,84 @@ def tile_list_two_hand_loads_kernel(
                     acc[:].rearrange("p (m u) -> p u m", u=4),
                     COPY, scale=note_t[:, 4 * blk + i : 4 * blk + i + 1],
                 )
-            woven = new(f"b_bf{blk}", [P, 4 * H], BF16)
+            woven = new(f"b_bf{blk}", [P, 4 * H], BF16, kb)
             weave(nc.scalar.copy, woven[:], rows[:], 4)
             quantize(b_w[:, H * blk : H * (blk + 1)], b_s[:, H * blk : H * (blk + 1)], woven[:])
 
-        left_hand(0, 0, "h2_2")
-        left_hand(1, 0, "h2_3")
+        left_half(0, 0, 75, 0)
+        left_half(1, 0, 91, 1)
+        note_turned = bank("note_turned", 7)
+        nc.tensor.transpose(note_turned[:, 0:P], note_rows[:], ident[:])
+        note_t = new("note_t", [P, 8], F32, 182.5)
+        nc.scalar.copy(note_t[:], note_turned[:, 0:8])
+        load_mix(0, 1, 68)
+        load_mix(1, 1, 76)
+        wg2_t = new("wg2_t", [P, 4, S], F32, 92)
+        for k in range(4):
+            nc.sync.dma_start(wg2_t[32 * k : 32 * (k + 1), :, :], wg2.rearrange("(q i) j -> q i j", i=4))
+        load_tempo(0)
         quantize_wr(0)
         quantize_wr(1)
-        left_hand(0, 1, "wr_raw1")
-        quantize_mix(0, 0)
-        left_hand(1, 1, "mix_raw00")
-        make_b(0)
-        left_hand(2, 0, "b_rows0")
-        quantize_mix(1, 0)
-        left_hand(3, 0, "mix_raw10")
-        make_b(1)
-        left_hand(2, 1, "b_rows1")
-        quantize_mix(0, 1)
-        quantize_mix(1, 1)
-        left_hand(3, 1, "mix_raw11")
+        load_tempo(1)
+        left_half(0, 1, 60, 0)
+        left_half(1, 1, 62, 1)
+        left_half(2, 0, 58, 0)
+        quantize_mix(0, 0, 120)
+        make_b(0, 64)
+        left_half(3, 0, 0, 1)
+        left_half(2, 1, 2, 0)
+        quantize_mix(1, 0, 4)
+        make_b(1, 148)
+        left_half(3, 1, 8, 1)
+        quantize_mix(0, 1, 12)
+        wo_w_raw = new("wo_w_raw", [P, N], I32, 176)
+        wo_s_raw = new("wo_s_raw", [P, N], U8, 178)
+        nc.gpsimd.memset(wo_s_raw[:].bitcast(I32), 0)
+        nc.sync.dma_start(wo_w_raw[:], wo_words[0].rearrange("p c i -> p (c i)").bitcast(I32))
+        load_scale_rows(nc.sync, wo_s_raw, wo_scales, 1)
 
-        page_b_slots = ["wr_raw0", "wr_raw1", "tab_s", "v_s_raw"]
-        page_b = [new(f"page_b{i}", [P, T2], F32, slot=page_b_slots[i]) for i in range(4)]
-        for page in page_b:
-            clear_page(page)
+        page_b = [new(f"page_b{i}", [P, T2], F32, [52, 60, 0, 8][i]) for i in range(4)]
+        for i in range(4):
+            clear_page(page_b[i])
 
-        wo_w = new("wo_w", [P, N], I32)
-        wo_s = new("wo_s", [P, N], U8)
+        wo_w = new("wo_w", [P, N], I32, 179)
+        wo_s = new("wo_s", [P, N], U8, 181)
         nc.vector.tensor_copy(wo_w[:].rearrange("p (i m) -> p i m", i=4), wo_w_raw[:].rearrange("p (m i) -> p i m", i=4))
         nc.vector.tensor_copy(wo_s[:].rearrange("p (i m) -> p i m", i=4), wo_s_raw[:].rearrange("p (m i) -> p i m", i=4))
 
-        h2 = [new(f"h2_{i}", [P, S], F32, slot=(f"v_w{i}" if i < 2 else f"h2_{i}")) for i in range(4)]
-        for h in range(2):
-            for i in range(4):
-                acc = bank("h2_acc", "acc")
-                for a in range(2):
-                    cols = slice(S * a + HALF * h, S * a + HALF * (h + 1))
-                    nc.tensor.matmul_mx(
-                        out=acc[:],
-                        lhsT=b_w[:, H * a + P * i : H * a + P * (i + 1)].bitcast(FP8X4),
-                        lhsT_scale=b_s[:, H * a + P * i : H * a + P * (i + 1)],
-                        rhs=mix_w[:, cols].bitcast(FP8X4),
-                        rhs_scale=mix_s[:, cols],
-                        start=(a == 0), stop=(a == 1),
-                    )
-                nc.scalar.copy(h2[i][:, HALF * h : HALF * (h + 1)], acc[:])
+        h2 = [new(f"h2_{i}", [P, S], F32, 124 + 4 * i) for i in range(4)]
 
-        wide_slots = ["mix_raw00", "mix_raw10", "mix_raw01", "mix_raw11"]
-        staging = ["wr_bf1", "mix_bf00", "b_bf0", "wr_bf0", "b_rows0", "b_rows1", "b_bf1", "mix_bf10"]
-        left_t = [new(f"left_t{c}", [P, 2, H], F32, slot=staging[c]) for c in range(CHUNKS)]
-        for w in range(T2 // WIDE):
-            tempo_t = new(f"tempo_t{w}", [P, 4, WIDE], F32, slot=wide_slots[w])
-            nc.sync.dma_start(tempo_t[:], tempo[:, WIDE * w : WIDE * (w + 1)].rearrange("(s p) t -> p s t", p=P))
+        def right_product(i, h):
+            acc = bank(f"h2_acc{i}{h}", 2 + i % 2)
+            for a in range(2):
+                cols = slice(S * a + HALF * h, S * a + HALF * (h + 1))
+                nc.tensor.matmul_mx(
+                    out=acc[:],
+                    lhsT=b_w[:, H * a + P * i : H * a + P * (i + 1)].bitcast(FP8X4),
+                    lhsT_scale=b_s[:, H * a + P * i : H * a + P * (i + 1)],
+                    rhs=mix_w[:, cols].bitcast(FP8X4),
+                    rhs_scale=mix_s[:, cols],
+                    start=(a == 0), stop=(a == 1),
+                )
+            nc.scalar.copy(h2[i][:, HALF * h : HALF * (h + 1)], acc[:])
+
+        def right_half(i, h):
+            right_product(i, h)
+            cols = slice(HALF * h, HALF * (h + 1))
+            nc.vector.tensor_tensor(
+                page_b[i][:].indirect(idx3[:, LIST_COLS * h : LIST_COLS * (h + 1)]), h2[i][:, cols], wg2_t[:, i, cols], MULT,
+            )
+
+        left_t = [new(f"left_t{c}", [P, 2, H], F32, 183 + 4 * c) for c in range(CHUNKS)]
+
+        def turn_left(w):
             for j in range(WIDE // P):
                 beat = WIDE * w + P * j
-                turned = bank("turned", "turn")
+                turned = bank(f"turned{w}{j}", 4 + j)
                 for s in range(4):
                     nc.tensor.matmul(turned[:, P * s : P * (s + 1)], page_a[s][:, beat : beat + P], ident[:],
                                      start=True, stop=False, is_transpose=True)
-                    nc.tensor.matmul(turned[:, P * s : P * (s + 1)], tempo_t[:, s, P * j : P * (j + 1)], ident[:],
+                    nc.tensor.matmul(turned[:, P * s : P * (s + 1)], tempo_t[w][:, s, P * j : P * (j + 1)], ident[:],
                                      start=False, stop=True, is_transpose=True)
                 nc.scalar.activation(
                     left_t[beat // CHUNK][:, (beat % CHUNK) // P, :].rearrange("p (i m) -> p i m", i=4),
@@ -272,25 +295,38 @@ def tile_list_two_hand_loads_kernel(
                     ABS,
                 )
 
-        page_a_slots = ["page_a0", "page_a1", "tab_w0", "tab_w1"]
-        right = [new(f"right{w}", [P, 4, WIDE], F32, slot=page_a_slots[w]) for w in range(T2 // WIDE)]
+        right_half(0, 0)
+        right_half(1, 0)
+        quantize_mix(1, 1, 68)
+        load_tempo(2)
+        load_tempo(3)
+        right_half(2, 0)
+        right_half(3, 0)
+        turn_left(0)
+        turn_left(1)
+        right_half(0, 1)
+        right_half(1, 1)
+        turn_left(2)
+        right_half(2, 1)
+        right_half(3, 1)
+        turn_left(3)
+
+        right = [new(f"right{w}", [P, 4, WIDE], F32, 16 + 8 * w) for w in range(T2 // WIDE)]
         for i in range(4):
-            page = page_b[i]
-            nc.vector.tensor_tensor(page[:].indirect(idx3[:]), h2[i][:], wg2_t[:, i, :], MULT)
             width = WIDE if i < 3 else CHUNK
             for c in range(0, T2, width):
-                nc.scalar.activation(right[c // WIDE][:, i, c % WIDE : c % WIDE + width], page[:, c : c + width], ABS)
+                nc.scalar.activation(right[c // WIDE][:, i, c % WIDE : c % WIDE + width], page_b[i][:, c : c + width], ABS)
 
-        y_w = new("y_w", [P, T2], I32)
-        y_s = new("y_s", [P, T2], U8)
+        y_w = new("y_w", [P, T2], I32, 157)
+        y_s = new("y_s", [P, T2], U8, 165)
         out_rows = out_0.rearrange("(p i) t -> p i t", i=4)
         out_words = out_1[0].rearrange("p m i -> p (m i)").bitcast(I32)
         z_bf, z_w, z_s, y_f, y_bf = {}, {}, {}, {}, {}
 
         def make_z(c):
-            z_bf[c] = new("z_bf", [P, 4 * CHUNK], BF16, bufs=2)
+            z_bf[c] = new(f"z_bf{c}", [P, 4 * CHUNK], BF16, 215 + 2 * (c % 2))
             for j in range(CHUNK // P):
-                back = bank("back", "turn")
+                back = bank(f"back{c}{j}", 4 + (2 * c + j) % 4)
                 for i in range(4):
                     nc.tensor.transpose(back[:, P * i : P * (i + 1)], left_t[c][:, j, P * i : P * (i + 1)], ident[:])
                 beat = CHUNK * c + P * j
@@ -302,12 +338,12 @@ def tile_list_two_hand_loads_kernel(
                 )
 
         def make_y(c):
-            z_w[c] = new("z_w", [P, CHUNK], U32, bufs=2)
-            z_s[c] = new("z_s", [P, CHUNK], U8, bufs=2)
+            z_w[c] = new(f"z_w{c}", [P, CHUNK], U32, 223 + c % 2)
+            z_s[c] = new(f"z_s{c}", [P, CHUNK], U8, 225 + 0.25 * (c % 2))
             quantize(z_w[c][:], z_s[c][:], z_bf[c][:])
-            y_f[c] = new(f"y_f{c}", [P, 4, CHUNK], F32, slot=wide_slots[c % 4])
+            y_f[c] = new(f"y_f{c}", [P, 4, CHUNK], F32, 68 + 4 * c if c < 6 else 84 + 4 * c)
             for pair in range(2):
-                acc = bank("y_acc", "acc")
+                acc = bank(f"y_acc{c}{pair}", (2 * c + pair) % 4)
                 for u in range(2):
                     i = 2 * pair + u
                     nc.tensor.matmul_mx(
@@ -322,7 +358,7 @@ def tile_list_two_hand_loads_kernel(
             nc.sync.dma_start(out_rows[:, :, CHUNK * c : CHUNK * (c + 1)], y_f[c][:])
 
         def round_y(c):
-            y_bf[c] = new("y_bf", [P, 4 * CHUNK], BF16, bufs=2)
+            y_bf[c] = new(f"y_bf{c}", [P, 4 * CHUNK], BF16, 219 + 2 * (c % 2))
             weave(nc.vector.tensor_copy if c % 2 == 1 else nc.scalar.copy, y_bf[c][:], y_f[c][:], 2)
 
         def planes_y(c):

@@ -68,19 +68,18 @@ def tile_list_two_hand_loads_kernel(
         tab_s = new("tab_s", [P, T], U8, 172)
         wl_s = new("wl_s", [P, 2 * H], U8, 178)
         v_s1 = new("v_s1", [P, S], U8, 175)
+        note_rows = new("note_rows", [P, P], F32, 182)
+        page_a = [new(f"page_a{s}", [P, T2], F32, 16 + 8 * s) for s in range(4)]
+        nc.gpsimd.memset(wl_s[:].bitcast(I32), 0)
         nc.vector.memset(tab_s[32:64, :].bitcast(I32), 0)
         nc.vector.memset(tab_s[64:128, :].bitcast(I32), 0)
-        nc.vector.memset(v_s1[:].bitcast(I32), 0)
-        nc.gpsimd.memset(wl_s[:].bitcast(I32), 0)
-        page_a = [new(f"page_a{s}", [P, T2], F32, 16 + 8 * s) for s in range(4)]
-        clear_page(page_a[0])
-        clear_page(page_a[1])
+        nc.vector.memset(page_a[0][:], 0.0)
+        nc.gpsimd.memset(v_s1[:].bitcast(I32), 0)
+        nc.gpsimd.memset(note_rows[:], 0.0)
         ident = new("ident", [P, P], F32, 181.5)
         make_identity(nc, ident[:])
-        note_rows = new("note_rows", [P, P], F32, 182)
-        nc.gpsimd.memset(note_rows[:], 0.0)
-        clear_page(page_a[2])
-        clear_page(page_a[3])
+        for s in range(1, 4):
+            clear_page(page_a[s])
 
         idx = lists.tile([P, S // 16], U16, name="idx")
         idx2 = lists.tile([P, S // 16], U16, name="idx2")
@@ -229,15 +228,15 @@ def tile_list_two_hand_loads_kernel(
         quantize_wr(0)
         quantize_wr(1)
         load_tempo(1)
-        left_half(0, 1, 60, 0)
-        left_half(1, 1, 62, 1)
-        left_half(2, 0, 58, 0)
+        left_half(0, 1, 52, 0)
+        left_half(1, 1, 54, 1)
+        left_half(2, 0, 56, 0)
         quantize_mix(0, 0, 120)
-        make_b(0, 64)
+        make_b(0, 58)
         left_half(3, 0, 0, 1)
         left_half(2, 1, 2, 0)
         quantize_mix(1, 0, 4)
-        make_b(1, 148)
+        make_b(1, 146)
         left_half(3, 1, 8, 1)
         quantize_mix(0, 1, 12)
         wo_w_raw = new("wo_w_raw", [P, N], I32, 176)
@@ -246,7 +245,7 @@ def tile_list_two_hand_loads_kernel(
         nc.sync.dma_start(wo_w_raw[:], wo_words[0].rearrange("p c i -> p (c i)").bitcast(I32))
         load_scale_rows(nc.sync, wo_s_raw, wo_scales, 1)
 
-        page_b = [new(f"page_b{i}", [P, T2], F32, [52, 60, 0, 8][i]) for i in range(4)]
+        page_b = [new(f"page_b{i}", [P, T2], F32, [52, 60, 140, 8][i]) for i in range(4)]
         for i in range(4):
             clear_page(page_b[i])
 

@@ -279,36 +279,30 @@ def tile_list_two_hand_loads_kernel(
 
         left_t = [new(f"left_t{c}", [P, 2, H], F32, 183 + 4 * c) for c in range(CHUNKS)]
 
-        def turn_left(w):
-            for j in range(WIDE // P):
-                beat = WIDE * w + P * j
-                turned = bank(f"turned{w}{j}", 4 + j)
-                for s in range(4):
-                    nc.tensor.matmul(turned[:, P * s : P * (s + 1)], page_a[s][:, beat : beat + P], ident[:],
-                                     start=True, stop=False, is_transpose=True)
-                    nc.tensor.matmul(turned[:, P * s : P * (s + 1)], tempo_t[w][:, s, P * j : P * (j + 1)], ident[:],
-                                     start=False, stop=True, is_transpose=True)
-                nc.scalar.activation(
-                    left_t[beat // CHUNK][:, (beat % CHUNK) // P, :].rearrange("p (i m) -> p i m", i=4),
-                    turned[:].rearrange("p (m i) -> p i m", i=4),
-                    ABS,
-                )
+        def turn_left(j):
+            beat = P * j
+            turned = bank(f"turned{j}", 4 + j % 4)
+            for s in range(4):
+                nc.tensor.matmul(turned[:, P * s : P * (s + 1)], page_a[s][:, beat : beat + P], ident[:],
+                                 start=True, stop=False, is_transpose=True)
+                nc.tensor.matmul(turned[:, P * s : P * (s + 1)], tempo_t[beat // WIDE][:, s, beat % WIDE : beat % WIDE + P], ident[:],
+                                 start=False, stop=True, is_transpose=True)
+            nc.scalar.activation(
+                left_t[beat // CHUNK][:, (beat % CHUNK) // P, :].rearrange("p (i m) -> p i m", i=4),
+                turned[:].rearrange("p (m i) -> p i m", i=4),
+                ABS,
+            )
 
-        right_half(0, 0)
-        right_half(1, 0)
         quantize_mix(1, 1, 68)
         load_tempo(2)
         load_tempo(3)
-        right_half(2, 0)
-        right_half(3, 0)
-        turn_left(0)
-        turn_left(1)
-        right_half(0, 1)
-        right_half(1, 1)
-        turn_left(2)
-        right_half(2, 1)
-        right_half(3, 1)
-        turn_left(3)
+        right_half(0, 0)
+        right_half(1, 0)
+        for step in range(8):
+            if step + 2 < 8:
+                right_half((step + 2) % 4, (step + 2) // 4)
+            turn_left(2 * step)
+            turn_left(2 * step + 1)
 
         right = [new(f"right{w}", [P, 4, WIDE], F32, 16 + 8 * w) for w in range(T2 // WIDE)]
         for i in range(4):

@@ -69,22 +69,21 @@ def tile_list_two_hand_loads_kernel(
         wl_s = new("wl_s", [P, 2 * H], U8, 178)
         v_s1 = new("v_s1", [P, S], U8, 175)
         note_rows = new("note_rows", [P, P], F32, 182)
-        page_a = [new(f"page_a{s}", [P, T2], F32, 16 + 8 * s) for s in range(4)]
+        page_a = [new(f"page_a{s}", [P, T2], F32, 24.5 + 8 * s) for s in range(2)]
         nc.gpsimd.memset(wl_s[:].bitcast(I32), 0)
         nc.vector.memset(tab_s[32:64, :].bitcast(I32), 0)
         nc.vector.memset(tab_s[64:128, :].bitcast(I32), 0)
         nc.vector.memset(page_a[0][:], 0.0)
+        nc.vector.memset(page_a[1][:], 0.0)
         nc.gpsimd.memset(v_s1[:].bitcast(I32), 0)
         nc.gpsimd.memset(note_rows[:], 0.0)
         ident = new("ident", [P, P], F32, 181.5)
         make_identity(nc, ident[:])
-        for s in range(1, 4):
-            clear_page(page_a[s])
 
         idx = lists.tile([P, S // 16], U16, name="idx")
         idx2 = lists.tile([P, S // 16], U16, name="idx2")
         idx3 = lists.tile([P, S // 16], U16, name="idx3")
-        tab_w = [new(f"tab_w{a}", [P, T], I32, 8 * a) for a in range(2)]
+        tab_w = [new(f"tab_w{a}", [P, T], I32, 8.5 * a) for a in range(2)]
         nc.sync.dma_start(idx[:], offs)
         nc.sync.dma_start(tab_s[0:32, :].bitcast(I32), tab_scales.rearrange("a r t -> (a r) t").bitcast(I32))
         load_scale_rows(nc.sync, wl_s, wl_scales, 2)
@@ -118,6 +117,8 @@ def tile_list_two_hand_loads_kernel(
             gather_words(a, 1)
 
         nc.sync.dma_start(idx2[:], offs2)
+        page_a.append(new("page_a2", [P, T2], F32, 16))
+        clear_page(page_a[2])
         wg1_t = new("wg1_t", [P, S], F32, 48)
         wr_raw = new("wr_raw", [P, 8 * H], F32, 52)
         wr_pass = [wr_raw[:, 4 * H * a : 4 * H * (a + 1)].rearrange("p (i r) -> p i r", i=4) for a in range(2)]
@@ -228,10 +229,12 @@ def tile_list_two_hand_loads_kernel(
         quantize_wr(0)
         quantize_wr(1)
         load_tempo(1)
+        page_a.append(new("page_a3", [P, T2], F32, 116))
+        clear_page(page_a[3])
         left_half(0, 1, 52, 0)
         left_half(1, 1, 54, 1)
         left_half(2, 0, 56, 0)
-        quantize_mix(0, 0, 120)
+        quantize_mix(0, 0, 226)
         make_b(0, 58)
         left_half(3, 0, 0, 1)
         left_half(2, 1, 2, 0)
@@ -304,7 +307,7 @@ def tile_list_two_hand_loads_kernel(
             turn_left(2 * step)
             turn_left(2 * step + 1)
 
-        right = [new(f"right{w}", [P, 4, WIDE], F32, 16 + 8 * w) for w in range(T2 // WIDE)]
+        right = [new(f"right{w}", [P, 4, WIDE], F32, [24.5, 32.5, 16, 116][w]) for w in range(T2 // WIDE)]
         for i in range(4):
             width = WIDE if i < 3 else CHUNK
             for c in range(0, T2, width):

@@ -69,14 +69,13 @@ def tile_list_two_hand_loads_kernel(
         wl_s = new("wl_s", [P, 2 * H], U8, 178)
         v_s1 = new("v_s1", [P, S], U8, 175)
         note_rows = new("note_rows", [P, P], F32, 182)
-        page_a = [new(f"page_a{s}", [P, T2], F32, 24.5 + 8 * s) for s in range(2)]
+        page_a = [new("page_a0", [P, T2], F32, 24)]
         nc.gpsimd.memset(wl_s[:].bitcast(I32), 0)
         nc.vector.memset(tab_s[32:64, :].bitcast(I32), 0)
         nc.vector.memset(tab_s[64:128, :].bitcast(I32), 0)
         nc.vector.memset(page_a[0][:], 0.0)
-        nc.vector.memset(page_a[1][:], 0.0)
-        nc.gpsimd.memset(v_s1[:].bitcast(I32), 0)
-        nc.gpsimd.memset(note_rows[:], 0.0)
+        nc.vector.memset(v_s1[:].bitcast(I32), 0)
+        nc.vector.memset(note_rows[:], 0.0)
         ident = new("ident", [P, P], F32, 181.5)
         make_identity(nc, ident[:])
 
@@ -117,8 +116,8 @@ def tile_list_two_hand_loads_kernel(
             gather_words(a, 1)
 
         nc.sync.dma_start(idx2[:], offs2)
-        page_a.append(new("page_a2", [P, T2], F32, 16))
-        clear_page(page_a[2])
+        page_a.append(new("page_a1", [P, T2], F32, 16))
+        clear_page(page_a[1])
         wg1_t = new("wg1_t", [P, S], F32, 48)
         wr_raw = new("wr_raw", [P, 8 * H], F32, 52)
         wr_pass = [wr_raw[:, 4 * H * a : 4 * H * (a + 1)].rearrange("p (i r) -> p i r", i=4) for a in range(2)]
@@ -181,7 +180,7 @@ def tile_list_two_hand_loads_kernel(
         b_s = new("b_s", [P, 2 * H], U8, 171)
 
         def quantize_wr(a):
-            woven = new(f"wr_bf{a}", [P, 4 * H], BF16, 112 + 4 * a)
+            woven = new(f"wr_bf{a}", [P, 4 * H], BF16, [112, 38][a])
             weave(nc.scalar.copy, woven[:], wr_pass[a], 2)
             quantize(wr_w[:, H * a : H * (a + 1)], wr_s[:, H * a : H * (a + 1)], woven[:])
 
@@ -229,7 +228,8 @@ def tile_list_two_hand_loads_kernel(
         quantize_wr(0)
         quantize_wr(1)
         load_tempo(1)
-        page_a.append(new("page_a3", [P, T2], F32, 116))
+        page_a.extend(new(f"page_a{s}", [P, T2], F32, 16 + 8 * s) for s in (2, 3))
+        clear_page(page_a[2])
         clear_page(page_a[3])
         left_half(0, 1, 52, 0)
         left_half(1, 1, 54, 1)
@@ -301,13 +301,12 @@ def tile_list_two_hand_loads_kernel(
         load_tempo(3)
         right_half(0, 0)
         right_half(1, 0)
-        for step in range(8):
-            if step + 2 < 8:
-                right_half((step + 2) % 4, (step + 2) // 4)
-            turn_left(2 * step)
-            turn_left(2 * step + 1)
+        for step in range(6):
+            right_half((step + 2) % 4, (step + 2) // 4)
+            for j in range(16 * step // 6, 16 * (step + 1) // 6):
+                turn_left(j)
 
-        right = [new(f"right{w}", [P, 4, WIDE], F32, [24.5, 32.5, 16, 116][w]) for w in range(T2 // WIDE)]
+        right = [new(f"right{w}", [P, 4, WIDE], F32, 16 + 8 * w) for w in range(T2 // WIDE)]
         for i in range(4):
             width = WIDE if i < 3 else CHUNK
             for c in range(0, T2, width):
@@ -322,7 +321,7 @@ def tile_list_two_hand_loads_kernel(
         def make_z(c):
             z_bf[c] = new(f"z_bf{c}", [P, 4 * CHUNK], BF16, 215 + 2 * (c % 2))
             for j in range(CHUNK // P):
-                back = bank(f"back{c}{j}", 4 + (2 * c + j) % 4)
+                back = bank(f"back{c}{j}", 2 + j if c == 0 else 4 + (2 * c - 2 + j) % 4)
                 for i in range(4):
                     nc.tensor.transpose(back[:, P * i : P * (i + 1)], left_t[c][:, j, P * i : P * (i + 1)], ident[:])
                 beat = CHUNK * c + P * j

@@ -87,9 +87,9 @@ def tile_list_two_hand_loads_kernel(
         nc.sync.dma_start(tab_s[0:32, :].bitcast(I32), tab_scales.rearrange("a r t -> (a r) t").bitcast(I32))
         load_scale_rows(nc.sync, wl_s, wl_scales, 2)
         wl_w = new("wl_w", [P, 2, 2 * H], U8, 176)
+        nc.sync.dma_start(tab_w[0][:], tab_words[0].rearrange("p t i -> p (t i)").bitcast(I32))
         nc.sync.dma_start(wl_w[:].bitcast(I32), wl_words.rearrange("a p n -> p a n").bitcast(I32))
-        for a in range(2):
-            nc.sync.dma_start(tab_w[a][:], tab_words[a].rearrange("p t i -> p (t i)").bitcast(I32))
+        nc.sync.dma_start(tab_w[1][:], tab_words[1].rearrange("p t i -> p (t i)").bitcast(I32))
 
         v_w = [new(f"v_w{a}", [P, S], U32, 124 + 4 * a) for a in range(2)]
         v_s_raw = new("v_s_raw", [P, S], U8, 51.5)
@@ -282,17 +282,23 @@ def tile_list_two_hand_loads_kernel(
 
         left_t = [new(f"left_t{c}", [P, 2, H], F32, 183 + 4 * c) for c in range(CHUNKS)]
 
-        def turn_left(j):
+        turned = {}
+
+        def turn_slice(j, s):
             beat = P * j
-            turned = bank(f"turned{j}", 4 + j % 4)
-            for s in range(4):
-                nc.tensor.matmul(turned[:, P * s : P * (s + 1)], page_a[s][:, beat : beat + P], ident[:],
-                                 start=True, stop=False, is_transpose=True)
-                nc.tensor.matmul(turned[:, P * s : P * (s + 1)], tempo_t[beat // WIDE][:, s, beat % WIDE : beat % WIDE + P], ident[:],
-                                 start=False, stop=True, is_transpose=True)
+            if s == 0:
+                turned[j] = bank(f"turned{j}", 4 + j % 4)
+            nc.tensor.matmul(turned[j][:, P * s : P * (s + 1)], page_a[s][:, beat : beat + P], ident[:],
+                             start=True, stop=False, is_transpose=True)
+            nc.tensor.matmul(turned[j][:, P * s : P * (s + 1)], tempo_t[beat // WIDE][:, s, beat % WIDE : beat % WIDE + P], ident[:],
+                             start=False, stop=True, is_transpose=True)
+
+        def turn_left(j):
+            for s in range(3 if j < 4 else 0, 4):
+                turn_slice(j, s)
             nc.scalar.activation(
-                left_t[beat // CHUNK][:, (beat % CHUNK) // P, :].rearrange("p (i m) -> p i m", i=4),
-                turned[:].rearrange("p (m i) -> p i m", i=4),
+                left_t[j // 2][:, j % 2, :].rearrange("p (i m) -> p i m", i=4),
+                turned[j][:].rearrange("p (m i) -> p i m", i=4),
                 ABS,
             )
 
@@ -301,74 +307,101 @@ def tile_list_two_hand_loads_kernel(
         load_tempo(3)
         right_half(0, 0)
         right_half(1, 0)
+        for j in range(4):
+            for s in range(3):
+                turn_slice(j, s)
         for step in range(6):
             right_half((step + 2) % 4, (step + 2) // 4)
             for j in range(16 * step // 6, 16 * (step + 1) // 6):
                 turn_left(j)
 
-        right = [new(f"right{w}", [P, 4, WIDE], F32, 16 + 8 * w) for w in range(T2 // WIDE)]
-        for i in range(4):
-            width = WIDE if i < 3 else CHUNK
-            for c in range(0, T2, width):
-                nc.scalar.activation(right[c // WIDE][:, i, c % WIDE : c % WIDE + width], page_b[i][:, c : c + width], ABS)
+        right = new("right", [P, 4 * T2], F32, 16)
+        right_rows = right[:].rearrange("p (i t) -> p i t", i=4)
+        left_n = {}
+
+        def turn_back(block, number):
+            back = bank(f"back{block}", number)
+            for i in range(4):
+                nc.tensor.transpose(back[:, P * i : P * (i + 1)], left_t[block // 2][:, block % 2, P * i : P * (i + 1)], ident[:])
+            return back
+
+        def copy_back(block):
+            c, j = divmod(block, 2)
+            if j == 0:
+                left_n[c] = new(f"left_n{c}", [P, 4, CHUNK], F32, [0, 4, 116, 120][c - 4])
+            back = turn_back(block, j)
+            nc.scalar.copy(left_n[c][:, :, P * j : P * (j + 1)], back[:].rearrange("p (i t) -> p i t", i=4))
+
+        copies = [[8,9],[10],[11]]
+        for i in range(3):
+            for block in copies[i]:
+                copy_back(block)
+            nc.scalar.activation(right_rows[:, i, :], page_b[i][:], ABS)
+        order = [0,1,2,3,4,5,6,7]
+        held = {}
+        for n, c in enumerate(order[:4]):
+            for j in range(2):
+                held[c, j] = turn_back(2 * c + j, (2 * n + 2 + j) % 8)
+        for start, width in [[0,256],[256,256],[512,512],[1024,1024]]:
+            nc.scalar.activation(right_rows[:, 3, start : start + width], page_b[3][:, start : start + width], ABS)
 
         y_w = new("y_w", [P, T2], I32, 157)
         y_s = new("y_s", [P, T2], U8, 165)
         out_rows = out_0.rearrange("(p i) t -> p i t", i=4)
         out_words = out_1[0].rearrange("p m i -> p (m i)").bitcast(I32)
-        z_bf, z_w, z_s, y_f, y_bf = {}, {}, {}, {}, {}
+        y_f = [new(f"y_f{w}", [P, 4, WIDE], F32, [68, 76, 84, 108][w]) for w in range(T2 // WIDE)]
 
-        def make_z(c):
-            z_bf[c] = new(f"z_bf{c}", [P, 4 * CHUNK], BF16, 215 + 2 * (c % 2))
-            for j in range(CHUNK // P):
-                back = bank(f"back{c}{j}", 2 + j if c == 0 else 4 + (2 * c - 2 + j) % 4)
-                for i in range(4):
-                    nc.tensor.transpose(back[:, P * i : P * (i + 1)], left_t[c][:, j, P * i : P * (i + 1)], ident[:])
-                beat = CHUNK * c + P * j
-                nc.vector.tensor_tensor(
-                    z_bf[c][:, 4 * P * j : 4 * P * (j + 1)].rearrange("p (c e i) -> p c i e", e=2, i=4),
-                    back[:].rearrange("p (i c e) -> p c i e", e=2, i=4),
-                    right[beat // WIDE][:, :, beat % WIDE : beat % WIDE + P].rearrange("p i (c e) -> p c i e", e=2),
-                    SUBTRACT,
-                )
+        def subtract(dst, left, beat, width):
+            nc.vector.tensor_tensor(
+                dst.rearrange("p (c e i) -> p c i e", e=2, i=4),
+                left.rearrange("p i (c e) -> p c i e", e=2),
+                right_rows[:, :, beat : beat + width].rearrange("p i (c e) -> p c i e", e=2),
+                SUBTRACT,
+            )
 
-        def make_y(c):
-            z_w[c] = new(f"z_w{c}", [P, CHUNK], U32, 223 + c % 2)
-            z_s[c] = new(f"z_s{c}", [P, CHUNK], U8, 225 + 0.25 * (c % 2))
-            quantize(z_w[c][:], z_s[c][:], z_bf[c][:])
-            y_f[c] = new(f"y_f{c}", [P, 4, CHUNK], F32, 68 + 4 * c if c < 6 else 84 + 4 * c)
+        def make_y(n, c):
+            beat = CHUNK * c
+            z_bf = new(f"z_bf{c}", [P, 4 * CHUNK], BF16, 131 if n == CHUNKS - 1 else 215 + 2 * (n % 3))
+            if c in left_n:
+                subtract(z_bf[:], left_n[c][:], beat, CHUNK)
+            else:
+                for j in range(2):
+                    if (c, j) not in held:
+                        held[c, j] = turn_back(2 * c + j, (2 * n + 2 + j) % 8)
+                    subtract(z_bf[:, 4 * P * j : 4 * P * (j + 1)], held[c, j][:].rearrange("p (i t) -> p i t", i=4), beat + P * j, P)
+            z_w = new(f"z_w{c}", [P, CHUNK], U32, 231 + n % 3)
+            z_s = new(f"z_s{c}", [P, CHUNK], U8, 235 + 0.25 * (n % 3))
+            quantize(z_w[:], z_s[:], z_bf[:])
+            rows = y_f[beat // WIDE][:, :, beat % WIDE : beat % WIDE + CHUNK]
             for pair in range(2):
-                acc = bank(f"y_acc{c}{pair}", (2 * c + pair) % 4)
+                acc = bank(f"y_acc{c}{pair}", (2 * n + 2 + pair) % 8)
                 for u in range(2):
                     i = 2 * pair + u
                     nc.tensor.matmul_mx(
                         out=acc[:, CHUNK * u : CHUNK * (u + 1)],
                         lhsT=wo_w[:, P * i : P * (i + 1)].bitcast(FP8X4),
                         lhsT_scale=wo_s[:, P * i : P * (i + 1)],
-                        rhs=z_w[c][:].bitcast(FP8X4),
-                        rhs_scale=z_s[c][:],
+                        rhs=z_w[:].bitcast(FP8X4),
+                        rhs_scale=z_s[:],
                         start=True, stop=True,
                     )
-                nc.scalar.copy(y_f[c][:, 2 * pair : 2 * pair + 2, :], acc[:].rearrange("p (u t) -> p u t", u=2))
-            nc.sync.dma_start(out_rows[:, :, CHUNK * c : CHUNK * (c + 1)], y_f[c][:])
+                nc.scalar.copy(rows[:, 2 * pair : 2 * pair + 2, :], acc[:].rearrange("p (u t) -> p u t", u=2))
+            nc.sync.dma_start(out_rows[:, :, beat : beat + CHUNK], rows)
 
-        def round_y(c):
-            y_bf[c] = new(f"y_bf{c}", [P, 4 * CHUNK], BF16, 219 + 2 * (c % 2))
-            weave(nc.vector.tensor_copy if c % 2 == 1 else nc.scalar.copy, y_bf[c][:], y_f[c][:], 2)
-
-        def planes_y(c):
-            cols = slice(CHUNK * c, CHUNK * (c + 1))
-            quantize(y_w[:, cols], y_s[:, cols], y_bf[c][:])
+        def planes_y(start, width, engine):
+            y_bf = new(f"y_bf{start}", [P, 4 * width], BF16, 124 + start // 128)
+            rows = y_f[start // WIDE][:, :, start % WIDE : start % WIDE + width]
+            if engine == "g":
+                nc.gpsimd.tensor_copy(y_bf[:].rearrange("p (t i) -> p t i", i=4), rows.rearrange("p i t -> p t i"))
+            else:
+                weave(nc.vector.tensor_copy if engine == "v" else nc.scalar.copy, y_bf[:], rows, 2)
+            cols = slice(start, start + width)
+            quantize(y_w[:, cols], y_s[:, cols], y_bf[:])
             nc.sync.dma_start(out_words[:, cols], y_w[:, cols])
 
-        make_z(0)
-        make_y(0)
-        for c in range(CHUNKS):
-            if c + 1 < CHUNKS:
-                make_z(c + 1)
-            round_y(c)
-            if c + 1 < CHUNKS:
-                make_y(c + 1)
-            planes_y(c)
+        for n, c in enumerate(order):
+            make_y(n, c)
+        for start, width, engine in [[0,256,"s"],[256,256,"s"],[512,512,"v"],[1024,512,"s"],[1536,256,"v"],[1792,256,"v"]]:
+            planes_y(start, width, engine)
         for q in range(4):
             nc.sync.dma_start(out_2[0, 4 * q : 4 * q + 4, :].bitcast(I32), y_s[32 * q : 32 * q + 4, :].bitcast(I32))

@@ -141,7 +141,7 @@ def tile_list_two_hand_loads_kernel(
 
         load_mix(0, 0, 0)
         load_mix(1, 0, 8)
-        tempo_kb = [84, 108, 68, 76]
+        tempo_kb = [84, 108, 8, 76]
         tempo_t = {}
 
         def load_tempo(w):
@@ -248,9 +248,9 @@ def tile_list_two_hand_loads_kernel(
         nc.sync.dma_start(wo_w_raw[:], wo_words[0].rearrange("p c i -> p (c i)").bitcast(I32))
         load_scale_rows(nc.sync, wo_s_raw, wo_scales, 1)
 
-        page_b = [new(f"page_b{i}", [P, T2], F32, [52, 60, 140, 8][i]) for i in range(4)]
-        for i in range(4):
-            clear_page(page_b[i])
+        page_b = [new(f"page_b{i}", [P, T2], F32, [52, 60, 140][i]) for i in range(3)]
+        for page in page_b:
+            clear_page(page)
 
         wo_w = new("wo_w", [P, N], I32, 179)
         wo_s = new("wo_s", [P, N], U8, 181)
@@ -303,6 +303,8 @@ def tile_list_two_hand_loads_kernel(
             )
 
         quantize_mix(1, 1, 68)
+        page_b.append(new("page_b3", [P, T2], F32, 68))
+        clear_page(page_b[3])
         load_tempo(2)
         load_tempo(3)
         right_half(0, 0)
@@ -317,39 +319,27 @@ def tile_list_two_hand_loads_kernel(
 
         right = new("right", [P, 4 * T2], F32, 16)
         right_rows = right[:].rearrange("p (i t) -> p i t", i=4)
-        left_n = {}
+        left_n = new("left_n", [P, 4, WIDE], F32, 0)
 
         def turn_back(block, number):
             back = bank(f"back{block}", number)
             for i in range(4):
                 nc.tensor.transpose(back[:, P * i : P * (i + 1)], left_t[block // 2][:, block % 2, P * i : P * (i + 1)], ident[:])
-            return back
+            return back[:].rearrange("p (i t) -> p i t", i=4)
 
-        def copy_back(block):
-            c, j = divmod(block, 2)
-            if j == 0:
-                left_n[c] = new(f"left_n{c}", [P, 4, CHUNK], F32, [0, 4, 116, 120][c - 4])
-            back = turn_back(block, j)
-            nc.scalar.copy(left_n[c][:, :, P * j : P * (j + 1)], back[:].rearrange("p (i t) -> p i t", i=4))
-
-        copies = [[8,9],[10],[11]]
-        for i in range(3):
-            for block in copies[i]:
-                copy_back(block)
+        for i, blocks in enumerate([[8,9],[10],[11]]):
+            for block in blocks:
+                nc.scalar.copy(left_n[:, :, P * (block - 8) : P * (block - 7)], turn_back(block, block % 2))
             nc.scalar.activation(right_rows[:, i, :], page_b[i][:], ABS)
-        order = [0,1,2,3,4,5,6,7]
-        held = {}
-        for n, c in enumerate(order[:4]):
-            for j in range(2):
-                held[c, j] = turn_back(2 * c + j, (2 * n + 2 + j) % 8)
-        for start, width in [[0,256],[256,256],[512,512],[1024,1024]]:
+        held = [turn_back(block, (2 + block) % 8) for block in range(8)]
+        for start, width in [[0,128],[128,384],[512,512],[1024,1024]]:
             nc.scalar.activation(right_rows[:, 3, start : start + width], page_b[3][:, start : start + width], ABS)
 
         y_w = new("y_w", [P, T2], I32, 157)
         y_s = new("y_s", [P, T2], U8, 165)
         out_rows = out_0.rearrange("(p i) t -> p i t", i=4)
         out_words = out_1[0].rearrange("p m i -> p (m i)").bitcast(I32)
-        y_f = [new(f"y_f{w}", [P, 4, WIDE], F32, [68, 76, 84, 108][w]) for w in range(T2 // WIDE)]
+        y_f = [new(f"y_f{w}", [P, 4, WIDE], F32, [8, 76, 84, 108][w]) for w in range(T2 // WIDE)]
 
         def subtract(dst, left, beat, width):
             nc.vector.tensor_tensor(
@@ -359,49 +349,52 @@ def tile_list_two_hand_loads_kernel(
                 SUBTRACT,
             )
 
-        def make_y(n, c):
-            beat = CHUNK * c
-            z_bf = new(f"z_bf{c}", [P, 4 * CHUNK], BF16, 131 if n == CHUNKS - 1 else 215 + 2 * (n % 3))
-            if c in left_n:
-                subtract(z_bf[:], left_n[c][:], beat, CHUNK)
+        def make_y(n, beat, width):
+            first = beat // P
+            z_bf = new(f"z_bf{n}", [P, 4 * width], BF16, 131.5 if beat + width == T2 else 215 + 4 * (n % 3))
+            if 8 <= first < 12:
+                subtract(z_bf[:], left_n[:, :, beat - 8 * P : beat - 8 * P + width], beat, width)
             else:
-                for j in range(2):
-                    if (c, j) not in held:
-                        held[c, j] = turn_back(2 * c + j, (2 * n + 2 + j) % 8)
-                    subtract(z_bf[:, 4 * P * j : 4 * P * (j + 1)], held[c, j][:].rearrange("p (i t) -> p i t", i=4), beat + P * j, P)
-            z_w = new(f"z_w{c}", [P, CHUNK], U32, 231 + n % 3)
-            z_s = new(f"z_s{c}", [P, CHUNK], U8, 235 + 0.25 * (n % 3))
+                for j in range(width // P):
+                    block = first + j
+                    left = held[block] if block < 8 else turn_back(block, (2 + block) % 8)
+                    subtract(z_bf[:, 4 * P * j : 4 * P * (j + 1)], left, beat + P * j, P)
+            z_w = new(f"z_w{n}", [P, width], U32, 227 + 2 * (n % 3))
+            z_s = new(f"z_s{n}", [P, width], U8, 233 + 0.5 * (n % 3))
             quantize(z_w[:], z_s[:], z_bf[:])
-            rows = y_f[beat // WIDE][:, :, beat % WIDE : beat % WIDE + CHUNK]
-            for pair in range(2):
-                acc = bank(f"y_acc{c}{pair}", (2 * n + 2 + pair) % 8)
-                for u in range(2):
-                    i = 2 * pair + u
+            rows = y_f[beat // WIDE][:, :, beat % WIDE : beat % WIDE + width]
+            side = WIDE // width
+            for group in range(width // P):
+                acc = bank(f"y_acc{n}{group}", (2 + first + group) % 8)
+                for u in range(side):
+                    i = side * group + u
                     nc.tensor.matmul_mx(
-                        out=acc[:, CHUNK * u : CHUNK * (u + 1)],
+                        out=acc[:, width * u : width * (u + 1)],
                         lhsT=wo_w[:, P * i : P * (i + 1)].bitcast(FP8X4),
                         lhsT_scale=wo_s[:, P * i : P * (i + 1)],
                         rhs=z_w[:].bitcast(FP8X4),
                         rhs_scale=z_s[:],
                         start=True, stop=True,
                     )
-                nc.scalar.copy(rows[:, 2 * pair : 2 * pair + 2, :], acc[:].rearrange("p (u t) -> p u t", u=2))
-            nc.sync.dma_start(out_rows[:, :, beat : beat + CHUNK], rows)
+                nc.scalar.copy(rows[:, side * group : side * (group + 1), :], acc[:].rearrange("p (u t) -> p u t", u=side))
+            nc.sync.dma_start(out_rows[:, :, beat : beat + width], rows)
+
+        stores = {768: 0, 1536: 768, 1792: 1536, 2048: 1792}
 
         def planes_y(start, width, engine):
-            y_bf = new(f"y_bf{start}", [P, 4 * width], BF16, 124 + start // 128)
+            y_bf = new(f"y_bf{start}", [P, 4 * width], BF16, 124 + start / 128)
             rows = y_f[start // WIDE][:, :, start % WIDE : start % WIDE + width]
-            if engine == "g":
-                nc.gpsimd.tensor_copy(y_bf[:].rearrange("p (t i) -> p t i", i=4), rows.rearrange("p i t -> p t i"))
-            else:
-                weave(nc.vector.tensor_copy if engine == "v" else nc.scalar.copy, y_bf[:], rows, 2)
+            weave(nc.vector.tensor_copy if engine == "v" else nc.scalar.copy, y_bf[:], rows, 2)
             cols = slice(start, start + width)
             quantize(y_w[:, cols], y_s[:, cols], y_bf[:])
-            nc.sync.dma_start(out_words[:, cols], y_w[:, cols])
+            if start + width in stores:
+                cols = slice(stores[start + width], start + width)
+                nc.sync.dma_start(out_words[:, cols], y_w[:, cols])
 
-        for n, c in enumerate(order):
-            make_y(n, c)
-        for start, width, engine in [[0,256,"s"],[256,256,"s"],[512,512,"v"],[1024,512,"s"],[1536,256,"v"],[1792,256,"v"]]:
+        widths = [128,128,256,256,256,256,256,256,256]
+        for n, width in enumerate(widths):
+            make_y(n, sum(widths[:n]), width)
+        for start, width, engine in [[0,256,"s"],[256,256,"s"],[512,256,"s"],[768,256,"v"],[1024,512,"v"],[1536,256,"s"],[1792,256,"v"]]:
             planes_y(start, width, engine)
         for q in range(4):
             nc.sync.dma_start(out_2[0, 4 * q : 4 * q + 4, :].bitcast(I32), y_s[32 * q : 32 * q + 4, :].bitcast(I32))

@@ -16,6 +16,7 @@ FP8X4 = mybir.dt.float8_e4m3fn_x4
 FP4X4 = mybir.dt.float4_e2m1fn_x4
 MULT = mybir.AluOpType.mult
 SUBTRACT = mybir.AluOpType.subtract
+ADD = mybir.AluOpType.add
 COPY = mybir.ActivationFunctionType.Copy
 ABS = mybir.ActivationFunctionType.Abs
 
@@ -327,15 +328,14 @@ def tile_list_two_hand_loads_kernel(
                 nc.tensor.transpose(back[:, P * i : P * (i + 1)], left_t[block // 2][:, block % 2, P * i : P * (i + 1)], ident[:])
             return back[:].rearrange("p (i t) -> p i t", i=4)
 
-        for i, blocks in enumerate([[8,9],[10],[11]]):
+        for i, blocks in enumerate([[2, 3], [4], [5]]):
             for block in blocks:
-                nc.scalar.copy(left_n[:, :, P * (block - 8) : P * (block - 7)], turn_back(block, block % 2))
+                nc.scalar.copy(left_n[:, :, P * (block - 2) : P * (block - 1)], turn_back(block, block % 2))
             nc.scalar.activation(right_rows[:, i, :], page_b[i][:], ABS)
-        held = [turn_back(block, (2 + block) % 8) for block in range(8)]
+        held = {block: turn_back(block, number) for block, number in zip([0, 1, 6, 7, 8, 9, 10, 11], [2, 3, 4, 5, 6, 7, 0, 1])}
         for start, width in [[0,128],[128,384],[512,512],[1024,1024]]:
             nc.scalar.activation(right_rows[:, 3, start : start + width], page_b[3][:, start : start + width], ABS)
 
-        y_w = new("y_w", [P, T2], I32, 157)
         y_s = new("y_s", [P, T2], U8, 165)
         out_rows = out_0.rearrange("(p i) t -> p i t", i=4)
         out_words = out_1[0].rearrange("p m i -> p (m i)").bitcast(I32)
@@ -349,23 +349,28 @@ def tile_list_two_hand_loads_kernel(
                 SUBTRACT,
             )
 
-        def make_y(n, beat, width):
+        z_bf = {}
+
+        def make_z(beat, width, kb):
+            z_bf[beat] = new(f"z_bf{beat}", [P, 4 * width], BF16, kb)
             first = beat // P
-            z_bf = new(f"z_bf{n}", [P, 4 * width], BF16, 131.5 if beat + width == T2 else 215 + 4 * (n % 3))
-            if 8 <= first < 12:
-                subtract(z_bf[:], left_n[:, :, beat - 8 * P : beat - 8 * P + width], beat, width)
+            if 2 <= first < 6:
+                subtract(z_bf[beat][:], left_n[:, :, beat - 2 * P : beat - 2 * P + width], beat, width)
             else:
                 for j in range(width // P):
-                    block = first + j
-                    left = held[block] if block < 8 else turn_back(block, (2 + block) % 8)
-                    subtract(z_bf[:, 4 * P * j : 4 * P * (j + 1)], left, beat + P * j, P)
-            z_w = new(f"z_w{n}", [P, width], U32, 227 + 2 * (n % 3))
-            z_s = new(f"z_s{n}", [P, width], U8, 233 + 0.5 * (n % 3))
-            quantize(z_w[:], z_s[:], z_bf[:])
+                    subtract(z_bf[beat][:, 4 * P * j : 4 * P * (j + 1)], held[first + j], beat + P * j, P)
+
+        made = []
+
+        def make_y(beat, width, numbers):
+            z_w = new(f"z_w{beat}", [P, width], U32, 227 + 2 * (len(made) % 3))
+            z_s = new(f"z_s{beat}", [P, width], U8, 233 + 0.5 * (len(made) % 3))
+            made.append(beat)
+            quantize(z_w[:], z_s[:], z_bf[beat][:])
             rows = y_f[beat // WIDE][:, :, beat % WIDE : beat % WIDE + width]
             side = WIDE // width
-            for group in range(width // P):
-                acc = bank(f"y_acc{n}{group}", (2 + first + group) % 8)
+            for group, number in enumerate(numbers):
+                acc = bank(f"y_acc{beat}_{group}", number)
                 for u in range(side):
                     i = side * group + u
                     nc.tensor.matmul_mx(
@@ -379,22 +384,69 @@ def tile_list_two_hand_loads_kernel(
                 nc.scalar.copy(rows[:, side * group : side * (group + 1), :], acc[:].rearrange("p (u t) -> p u t", u=side))
             nc.sync.dma_start(out_rows[:, :, beat : beat + width], rows)
 
-        stores = {768: 0, 1536: 768, 1792: 1536, 2048: 1792}
+        y_bf = {}
 
-        def planes_y(start, width, engine):
-            y_bf = new(f"y_bf{start}", [P, 4 * width], BF16, 124 + start / 128)
-            rows = y_f[start // WIDE][:, :, start % WIDE : start % WIDE + width]
-            weave(nc.vector.tensor_copy if engine == "v" else nc.scalar.copy, y_bf[:], rows, 2)
+        def y_rows(start, width):
+            return y_f[start // WIDE][:, :, start % WIDE : start % WIDE + width]
+
+        def round_y(engine_copy, start, width, kb):
+            y_bf[start] = new(f"y_bf{start}", [P, 4 * width], BF16, kb)
+            weave(engine_copy, y_bf[start][:], y_rows(start, width), 2)
+
+        def round_y_aside(start, width, kb):
+            y_bf[start] = new(f"y_bf{start}", [P, 4 * width], BF16, kb)
+            nc.gpsimd.tensor_scalar(
+                y_bf[start][:].rearrange("p (t i) -> p t i", i=4), y_rows(start, width).rearrange("p i t -> p t i"),
+                1.0, 0.0, MULT, ADD,
+            )
+
+        stores = {512: 0, 1024: 512, 1536: 1024, 1792: 1536, 2048: 1792}
+
+        def planes_y(start, width):
             cols = slice(start, start + width)
-            quantize(y_w[:, cols], y_s[:, cols], y_bf[:])
+            quantize(y_w[:, cols], y_s[:, cols], y_bf[start][:])
             if start + width in stores:
                 cols = slice(stores[start + width], start + width)
                 nc.sync.dma_start(out_words[:, cols], y_w[:, cols])
 
-        widths = [128,128,256,256,256,256,256,256,256]
-        for n, width in enumerate(widths):
-            make_y(n, sum(widths[:n]), width)
-        for start, width, engine in [[0,256,"s"],[256,256,"s"],[512,256,"s"],[768,256,"v"],[1024,512,"v"],[1536,256,"s"],[1792,256,"v"]]:
-            planes_y(start, width, engine)
+        make_z(0, P, 215)
+        make_z(128, P, 216)
+        make_y(0, P, [2])
+        make_z(256, CHUNK, 217)
+        make_y(128, P, [3])
+        make_z(512, CHUNK, 219)
+        make_y(256, CHUNK, [2, 3])
+        make_y(512, CHUNK, [4, 5])
+        round_y_aside(0, CHUNK, 219)
+        make_z(768, CHUNK, 221)
+        make_z(1024, CHUNK, 223)
+        make_y(768, CHUNK, [6, 7])
+        held[12] = turn_back(12, 2)
+        held[13] = turn_back(13, 3)
+        make_y(1024, CHUNK, [0, 1])
+        round_y_aside(256, CHUNK, 223)
+        held[14] = turn_back(14, 4)
+        held[15] = turn_back(15, 5)
+        make_z(1280, CHUNK, 157)
+        make_z(1536, CHUNK, 124)
+        y_w = new("y_w", [P, T2], I32, 157)
+        make_y(1280, CHUNK, [6, 7])
+        round_y(nc.scalar.copy, 768, CHUNK, 128)
+        planes_y(0, CHUNK)
+        planes_y(256, CHUNK)
+        make_y(1536, CHUNK, [2, 3])
+        round_y_aside(512, P, 223)
+        round_y(nc.scalar.copy, 640, P, 126)
+        make_z(1792, CHUNK, 133)
+        make_y(1792, CHUNK, [4, 5])
+        round_y(nc.scalar.copy, 1536, CHUNK, 136)
+        round_y(nc.vector.tensor_copy, 1024, WIDE, 130)
+        planes_y(512, P)
+        planes_y(640, P)
+        planes_y(768, CHUNK)
+        planes_y(1024, WIDE)
+        round_y(nc.vector.tensor_copy, 1792, CHUNK, 138)
+        planes_y(1536, CHUNK)
+        planes_y(1792, CHUNK)
         for q in range(4):
             nc.sync.dma_start(out_2[0, 4 * q : 4 * q + 4, :].bitcast(I32), y_s[32 * q : 32 * q + 4, :].bitcast(I32))

@@ -253,12 +253,7 @@ def tile_list_two_hand_loads_kernel(
         for page in page_b:
             clear_page(page)
 
-        wo_w = new("wo_w", [P, N], I32, 179)
-        wo_s = new("wo_s", [P, N], U8, 181)
-        nc.vector.tensor_copy(wo_w[:].rearrange("p (i m) -> p i m", i=4), wo_w_raw[:].rearrange("p (m i) -> p i m", i=4))
-        nc.vector.tensor_copy(wo_s[:].rearrange("p (i m) -> p i m", i=4), wo_s_raw[:].rearrange("p (m i) -> p i m", i=4))
-
-        h2 = [new(f"h2_{i}", [P, S], F32, 124 + 4 * i) for i in range(4)]
+        h2 = {}
 
         def right_product(i, h):
             acc = bank(f"h2_acc{i}{h}", 2 + i % 2)
@@ -272,13 +267,14 @@ def tile_list_two_hand_loads_kernel(
                     rhs_scale=mix_s[:, cols],
                     start=(a == 0), stop=(a == 1),
                 )
-            nc.scalar.copy(h2[i][:, HALF * h : HALF * (h + 1)], acc[:])
+            h2[i, h] = new(f"h2_{i}{h}", [P, HALF], F32, 179.5 if (i, h) == (3, 1) else 124 + 4 * i + 2 * h)
+            nc.scalar.copy(h2[i, h][:], acc[:])
 
         def right_half(i, h):
             right_product(i, h)
             cols = slice(HALF * h, HALF * (h + 1))
             nc.vector.tensor_tensor(
-                page_b[i][:].indirect(idx3[:, LIST_COLS * h : LIST_COLS * (h + 1)]), h2[i][:, cols], wg2_t[:, i, cols], MULT,
+                page_b[i][:].indirect(idx3[:, LIST_COLS * h : LIST_COLS * (h + 1)]), h2[i, h][:], wg2_t[:, i, cols], MULT,
             )
 
         left_t = [new(f"left_t{c}", [P, 2, H], F32, 183 + 4 * c) for c in range(CHUNKS)]
@@ -335,6 +331,11 @@ def tile_list_two_hand_loads_kernel(
         held = {block: turn_back(block, number) for block, number in zip([0, 1, 6, 7, 8, 9, 10, 11], [2, 3, 4, 5, 6, 7, 0, 1])}
         for start, width in [[0,128],[128,384],[512,512],[1024,1024]]:
             nc.scalar.activation(right_rows[:, 3, start : start + width], page_b[3][:, start : start + width], ABS)
+
+        wo_w = new("wo_w", [P, N], I32, 179)
+        wo_s = new("wo_s", [P, N], U8, 181)
+        nc.vector.tensor_copy(wo_w[:].rearrange("p (i m) -> p i m", i=4), wo_w_raw[:].rearrange("p (m i) -> p i m", i=4))
+        nc.gpsimd.tensor_copy(wo_s[:].rearrange("p (i m) -> p i m", i=4), wo_s_raw[:].rearrange("p (m i) -> p i m", i=4))
 
         y_s = new("y_s", [P, T2], U8, 165)
         out_rows = out_0.rearrange("(p i) t -> p i t", i=4)

from contextlib import ExitStack

import concourse.mybir as mybir
from concourse.masks import make_identity

K, H, N, T, S, T2 = 1024, 512, 512, 2048, 1024, 2048
FLOPS = 2 * (K * H * S + S * K * H + S * H * S + H * N * T2)

F32 = mybir.dt.float32
BF16 = mybir.dt.bfloat16
I32 = mybir.dt.int32
U32 = mybir.dt.uint32
U16 = mybir.dt.uint16
U8 = mybir.dt.uint8
FP8X4 = mybir.dt.float8_e4m3fn_x4
FP4X4 = mybir.dt.float4_e2m1fn_x4
MULT = mybir.AluOpType.mult
SUBTRACT = mybir.AluOpType.subtract
ADD = mybir.AluOpType.add
COPY = mybir.ActivationFunctionType.Copy
ABS = mybir.ActivationFunctionType.Abs

P = 128
KB = 1024
BANK = 2048
HALF = 512
LIST_COLS = HALF // 16
CHUNK = 256
CHUNKS = T2 // CHUNK
WIDE = 512


def tile_list_two_hand_loads_kernel(
    tc, tab_words, tab_scales, offs, offs2, offs3, wl_words, wl_scales, wr, note, mix,
    wg1, wg2, tempo, wo_words, wo_scales, out_0, out_1, out_2,
):
    nc = tc.nc
    with ExitStack() as ctx:
        lists = ctx.enter_context(tc.tile_pool(name="lists", bufs=1))
        sb = ctx.enter_context(tc.tile_pool(name="sb", bufs=1))
        psum = ctx.enter_context(tc.psum_pool(name="psum", bufs=1))

        def new(name, shape, dtype, kb):
            return sb.tile(shape, dtype, name=name, tag=name, align_bytes=64, offset=int(kb * KB))

        def bank(name, number):
            return psum.tile([P, 512], F32, name=name, tag=name, offset=number * BANK)

        def load_scale_rows(queue, tile, src, passes):
            for q in range(4):
                queue.dma_start(
                    tile[32 * q : 32 * q + 4, :].bitcast(I32).rearrange("p (a c) -> p a c", a=passes),
                    src[:, 4 * q : 4 * q + 4, :].rearrange("a r c -> r a c").bitcast(I32),
                )

        def weave(engine_copy, dst, src, run):
            engine_copy(
                dst.rearrange("p (c e i) -> p c i e", e=run, i=4),
                src.rearrange("p i (c e) -> p c i e", e=run),
            )

        def quantize(codes, scales, values):
            nc.vector.quantize_mx(out=codes.bitcast(FP8X4), scales=scales, in_=values)

        def clear_page(page):
            for c in range(0, T2, 512):
                nc.gpsimd.memset(page[:, c : c + 512], 0.0)

        tab_s = new("tab_s", [P, T], U8, 172)
        wl_s = new("wl_s", [P, 2 * H], U8, 178)
        v_s1 = new("v_s1", [P, S], U8, 175)
        note_rows = new("note_rows", [P, P], F32, 182)
        page_a = [new("page_a0", [P, T2], F32, 24)]
        nc.gpsimd.memset(wl_s[:].bitcast(I32), 0)
        nc.vector.memset(tab_s[32:64, :].bitcast(I32), 0)
        nc.vector.memset(tab_s[64:128, :].bitcast(I32), 0)
        nc.vector.memset(page_a[0][:], 0.0)
        nc.vector.memset(v_s1[:].bitcast(I32), 0)
        nc.vector.memset(note_rows[:], 0.0)
        ident = new("ident", [P, P], F32, 181.5)
        make_identity(nc, ident[:])

        idx = lists.tile([P, S // 16], U16, name="idx")
        idx2 = lists.tile([P, S // 16], U16, name="idx2")
        idx3 = lists.tile([P, S // 16], U16, name="idx3")
        tab_w = [new(f"tab_w{a}", [P, T], I32, 8.5 * a) for a in range(2)]
        nc.sync.dma_start(idx[:], offs)
        nc.sync.dma_start(tab_s[0:32, :].bitcast(I32), tab_scales.rearrange("a r t -> (a r) t").bitcast(I32))
        load_scale_rows(nc.sync, wl_s, wl_scales, 2)
        wl_w = new("wl_w", [P, 2, 2 * H], U8, 176)
        nc.sync.dma_start(tab_w[0][:], tab_words[0].rearrange("p t i -> p (t i)").bitcast(I32))
        nc.sync.dma_start(wl_w[:].bitcast(I32), wl_words.rearrange("a p n -> p a n").bitcast(I32))
        nc.sync.dma_start(tab_w[1][:], tab_words[1].rearrange("p t i -> p (t i)").bitcast(I32))

        v_w = [new(f"v_w{a}", [P, S], U32, 124 + 4 * a) for a in range(2)]
        v_s_raw = new("v_s_raw", [P, S], U8, 51.5)
        v_s0 = new("v_s0", [P, S], U8, 174)
        v_s = [v_s0, v_s1]

        def gather_words(a, h):
            nc.vector.tensor_copy(
                v_w[a][:, HALF * h : HALF * (h + 1)].rearrange("p (i g q) -> p g i q", i=4, q=8),
                tab_w[a][:].bitcast(U32).indirect(idx[:, LIST_COLS * h : LIST_COLS * (h + 1)]),
            )

        nc.vector.tensor_copy(v_s_raw[:], tab_s[:].indirect(idx[:]))
        nc.vector.tensor_copy(
            v_s0[:].bitcast(I32).rearrange("p (b i g w) -> p b g i w", i=4, g=16, w=2),
            v_s_raw[:].bitcast(I32).rearrange("p (b g i w) -> p b g i w", i=4, g=16, w=2),
        )
        for a in range(2):
            for q in range(1 - a, 4):
                row = 16 * a + 4 * q
                nc.sync.dma_start(v_s[a][32 * q : 32 * q + 4, :].bitcast(I32), v_s0[row : row + 4, :].bitcast(I32))
        for a in range(2):
            gather_words(a, 0)
            gather_words(a, 1)

        nc.sync.dma_start(idx2[:], offs2)
        page_a.append(new("page_a1", [P, T2], F32, 16))
        clear_page(page_a[1])
        wg1_t = new("wg1_t", [P, S], F32, 48)
        wr_raw = new("wr_raw", [P, 8 * H], F32, 52)
        wr_pass = [wr_raw[:, 4 * H * a : 4 * H * (a + 1)].rearrange("p (i r) -> p i r", i=4) for a in range(2)]
        nc.sync.dma_start(wg1_t[:, 0:HALF], wg1[:, 0:HALF])
        for a in range(2):
            nc.sync.dma_start(
                note_rows[4 * a : 4 * a + 4, :].rearrange("i (g q) -> i g q", q=8),
                note[512 * a : 512 * (a + 1)].rearrange("(g i q) -> i g q", i=4, q=8),
            )
        for a in range(2):
            nc.sync.dma_start(wr_pass[a], wr[512 * a : 512 * (a + 1), :].rearrange("(p i) r -> p i r", i=4))
        nc.sync.dma_start(wg1_t[:, HALF:S], wg1[:, HALF:S])
        nc.sync.dma_start(idx3[:], offs3)
        mix_raw = {}

        def load_mix(a, h, kb):
            mix_raw[a, h] = new(f"mix_raw{a}{h}", [P, 4, HALF], F32, kb)
            rows = mix[512 * a : 512 * (a + 1), HALF * h : HALF * (h + 1)].rearrange("(g i q) j -> i g q j", i=4, q=8)
            for i in range(4):
                nc.sync.dma_start(mix_raw[a, h][:, i, :], rows[i])

        load_mix(0, 0, 0)
        load_mix(1, 0, 8)
        tempo_kb = [84, 108, 8, 76]
        tempo_t = {}

        def load_tempo(w):
            tempo_t[w] = new(f"tempo_t{w}", [P, 4, WIDE], F32, tempo_kb[w])
            nc.sync.dma_start(tempo_t[w][:], tempo[:, WIDE * w : WIDE * (w + 1)].rearrange("(s p) t -> p s t", p=P))

        def left_product(s, h, number, dst):
            acc = bank(f"left_acc{s}{h}", number)
            for a in range(2):
                nc.tensor.matmul_mx(
                    out=acc[:],
                    lhsT=wl_w[:, a, 2 * P * s : 2 * P * (s + 1)].bitcast(FP4X4),
                    lhsT_scale=wl_s[:, H * a + P * s : H * a + P * (s + 1)],
                    rhs=v_w[a][:, HALF * h : HALF * (h + 1)].bitcast(FP8X4),
                    rhs_scale=v_s[a][:, HALF * h : HALF * (h + 1)],
                    start=(a == 0), stop=(a == 1),
                )
            nc.scalar.copy(
                dst.rearrange("p (g i q) -> p g i q", i=4, q=8),
                acc[:].rearrange("p (i g q) -> p g i q", i=4, q=8),
            )

        def left_half(s, h, kb, number):
            h1 = new(f"h1_{s}{h}", [P, HALF], F32, kb)
            left_product(s, h, number, h1[:])
            nc.vector.tensor_tensor(
                page_a[s][:].indirect(idx2[:, LIST_COLS * h : LIST_COLS * (h + 1)]),
                h1[:], wg1_t[:, HALF * h : HALF * (h + 1)], MULT,
            )

        wr_w = new("wr_w", [P, 2 * H], U32, 152)
        wr_s = new("wr_s", [P, 2 * H], U8, 156)
        mix_w = new("mix_w", [P, 2 * S], U32, 157)
        mix_s = new("mix_s", [P, 2 * S], U8, 165)
        b_w = new("b_w", [P, 2 * H], U32, 167)
        b_s = new("b_s", [P, 2 * H], U8, 171)

        def quantize_wr(a):
            woven = new(f"wr_bf{a}", [P, 4 * H], BF16, [112, 38][a])
            weave(nc.scalar.copy, woven[:], wr_pass[a], 2)
            quantize(wr_w[:, H * a : H * (a + 1)], wr_s[:, H * a : H * (a + 1)], woven[:])

        def quantize_mix(a, h, kb):
            woven = new(f"mix_bf{a}{h}", [P, 4 * HALF], BF16, kb)
            weave(nc.scalar.copy, woven[:], mix_raw[a, h][:], 2)
            cols = slice(S * a + HALF * h, S * a + HALF * (h + 1))
            quantize(mix_w[:, cols], mix_s[:, cols], woven[:])

        def make_b(blk, kb):
            rows = new(f"b_rows{blk}", [P, 4, H], BF16, 1 + 8 * blk)
            for i in range(4):
                acc = bank(f"b_acc{blk}{i}", 2 + i)
                first = HALF * blk + P * i
                for a in range(2):
                    nc.tensor.matmul_mx(
                        out=acc[:],
                        lhsT=v_w[a][:, first : first + P].bitcast(FP8X4),
                        lhsT_scale=v_s[a][:, first : first + P],
                        rhs=wr_w[:, H * a : H * (a + 1)].bitcast(FP8X4),
                        rhs_scale=wr_s[:, H * a : H * (a + 1)],
                        start=(a == 0), stop=(a == 1),
                    )
                nc.scalar.activation(
                    rows[:, i, :].rearrange("p (u m) -> p u m", u=4),
                    acc[:].rearrange("p (m u) -> p u m", u=4),
                    COPY, scale=note_t[:, 4 * blk + i : 4 * blk + i + 1],
                )
            woven = new(f"b_bf{blk}", [P, 4 * H], BF16, kb)
            weave(nc.scalar.copy, woven[:], rows[:], 4)
            quantize(b_w[:, H * blk : H * (blk + 1)], b_s[:, H * blk : H * (blk + 1)], woven[:])

        left_half(0, 0, 75, 0)
        left_half(1, 0, 91, 1)
        note_turned = bank("note_turned", 7)
        nc.tensor.transpose(note_turned[:, 0:P], note_rows[:], ident[:])
        note_t = new("note_t", [P, 8], F32, 182.5)
        nc.scalar.copy(note_t[:], note_turned[:, 0:8])
        load_mix(0, 1, 68)
        load_mix(1, 1, 76)
        wg2_t = new("wg2_t", [P, 4, S], F32, 92)
        for k in range(4):
            nc.sync.dma_start(wg2_t[32 * k : 32 * (k + 1), :, :], wg2.rearrange("(q i) j -> q i j", i=4))
        load_tempo(0)
        quantize_wr(0)
        quantize_wr(1)
        load_tempo(1)
        page_a.extend(new(f"page_a{s}", [P, T2], F32, 16 + 8 * s) for s in (2, 3))
        clear_page(page_a[2])
        clear_page(page_a[3])
        left_half(0, 1, 52, 0)
        left_half(1, 1, 54, 1)
        left_half(2, 0, 56, 0)
        quantize_mix(0, 0, 226)
        make_b(0, 58)
        left_half(3, 0, 0, 1)
        left_half(2, 1, 2, 0)
        quantize_mix(1, 0, 4)
        make_b(1, 146)
        left_half(3, 1, 8, 1)
        quantize_mix(0, 1, 12)
        wo_w_raw = new("wo_w_raw", [P, N], I32, 176)
        wo_s_raw = new("wo_s_raw", [P, N], U8, 178)
        nc.gpsimd.memset(wo_s_raw[:].bitcast(I32), 0)
        nc.sync.dma_start(wo_w_raw[:], wo_words[0].rearrange("p c i -> p (c i)").bitcast(I32))
        load_scale_rows(nc.sync, wo_s_raw, wo_scales, 1)

        page_b = [new(f"page_b{i}", [P, T2], F32, [52, 60, 140][i]) for i in range(3)]
        for page in page_b:
            clear_page(page)

        h2 = {}

        def right_product(i, h):
            acc = bank(f"h2_acc{i}{h}", 2 + i % 2)
            for a in range(2):
                cols = slice(S * a + HALF * h, S * a + HALF * (h + 1))
                nc.tensor.matmul_mx(
                    out=acc[:],
                    lhsT=b_w[:, H * a + P * i : H * a + P * (i + 1)].bitcast(FP8X4),
                    lhsT_scale=b_s[:, H * a + P * i : H * a + P * (i + 1)],
                    rhs=mix_w[:, cols].bitcast(FP8X4),
                    rhs_scale=mix_s[:, cols],
                    start=(a == 0), stop=(a == 1),
                )
            h2[i, h] = new(f"h2_{i}{h}", [P, HALF], F32, 179.5 if (i, h) == (3, 1) else 124 + 4 * i + 2 * h)
            nc.scalar.copy(h2[i, h][:], acc[:])

        def right_half(i, h):
            right_product(i, h)
            cols = slice(HALF * h, HALF * (h + 1))
            nc.vector.tensor_tensor(
                page_b[i][:].indirect(idx3[:, LIST_COLS * h : LIST_COLS * (h + 1)]), h2[i, h][:], wg2_t[:, i, cols], MULT,
            )

        left_t = [new(f"left_t{c}", [P, 2, H], F32, 183 + 4 * c) for c in range(CHUNKS)]

        turned = {}

        def turn_slice(j, s):
            beat = P * j
            if s == 0:
                turned[j] = bank(f"turned{j}", 4 + j % 4)
            nc.tensor.matmul(turned[j][:, P * s : P * (s + 1)], page_a[s][:, beat : beat + P], ident[:],
                             start=True, stop=False, is_transpose=True)
            nc.tensor.matmul(turned[j][:, P * s : P * (s + 1)], tempo_t[beat // WIDE][:, s, beat % WIDE : beat % WIDE + P], ident[:],
                             start=False, stop=True, is_transpose=True)

        def turn_left(j):
            for s in range(3 if j < 4 else 0, 4):
                turn_slice(j, s)
            nc.scalar.activation(
                left_t[j // 2][:, j % 2, :].rearrange("p (i m) -> p i m", i=4),
                turned[j][:].rearrange("p (m i) -> p i m", i=4),
                ABS,
            )

        quantize_mix(1, 1, 68)
        page_b.append(new("page_b3", [P, T2], F32, 68))
        clear_page(page_b[3])
        load_tempo(2)
        load_tempo(3)
        right_half(0, 0)
        right_half(1, 0)
        for j in range(4):
            for s in range(3):
                turn_slice(j, s)
        for step in range(6):
            right_half((step + 2) % 4, (step + 2) // 4)
            for j in range(16 * step // 6, 16 * (step + 1) // 6):
                turn_left(j)

        right = new("right", [P, 4 * T2], F32, 16)
        right_rows = right[:].rearrange("p (i t) -> p i t", i=4)
        left_n = new("left_n", [P, 4, WIDE], F32, 0)

        def turn_back(block, number):
            back = bank(f"back{block}", number)
            for i in range(4):
                nc.tensor.transpose(back[:, P * i : P * (i + 1)], left_t[block // 2][:, block % 2, P * i : P * (i + 1)], ident[:])
            return back[:].rearrange("p (i t) -> p i t", i=4)

        for i, blocks in enumerate([[2, 3], [4], [5]]):
            for block in blocks:
                nc.scalar.copy(left_n[:, :, P * (block - 2) : P * (block - 1)], turn_back(block, block % 2))
            nc.scalar.activation(right_rows[:, i, :], page_b[i][:], ABS)
        held = {block: turn_back(block, number) for block, number in zip([0, 1, 6, 7, 8, 9, 10, 11], [2, 3, 4, 5, 6, 7, 0, 1])}
        for start, width in [[0,128],[128,384],[512,512],[1024,1024]]:
            nc.scalar.activation(right_rows[:, 3, start : start + width], page_b[3][:, start : start + width], ABS)

        wo_w = new("wo_w", [P, N], I32, 179)
        wo_s = new("wo_s", [P, N], U8, 181)
        nc.vector.tensor_copy(wo_w[:].rearrange("p (i m) -> p i m", i=4), wo_w_raw[:].rearrange("p (m i) -> p i m", i=4))
        nc.gpsimd.tensor_copy(wo_s[:].rearrange("p (i m) -> p i m", i=4), wo_s_raw[:].rearrange("p (m i) -> p i m", i=4))

        y_s = new("y_s", [P, T2], U8, 165)
        out_rows = out_0.rearrange("(p i) t -> p i t", i=4)
        out_words = out_1[0].rearrange("p m i -> p (m i)").bitcast(I32)
        y_f = [new(f"y_f{w}", [P, 4, WIDE], F32, [8, 76, 84, 108][w]) for w in range(T2 // WIDE)]

        def subtract(dst, left, beat, width):
            nc.vector.tensor_tensor(
                dst.rearrange("p (c e i) -> p c i e", e=2, i=4),
                left.rearrange("p i (c e) -> p c i e", e=2),
                right_rows[:, :, beat : beat + width].rearrange("p i (c e) -> p c i e", e=2),
                SUBTRACT,
            )

        z_bf = {}

        def make_z(beat, width, kb):
            z_bf[beat] = new(f"z_bf{beat}", [P, 4 * width], BF16, kb)
            first = beat // P
            if 2 <= first < 6:
                subtract(z_bf[beat][:], left_n[:, :, beat - 2 * P : beat - 2 * P + width], beat, width)
            else:
                for j in range(width // P):
                    subtract(z_bf[beat][:, 4 * P * j : 4 * P * (j + 1)], held[first + j], beat + P * j, P)

        made = []

        def make_y(beat, width, numbers):
            z_w = new(f"z_w{beat}", [P, width], U32, 227 + 2 * (len(made) % 3))
            z_s = new(f"z_s{beat}", [P, width], U8, 233 + 0.5 * (len(made) % 3))
            made.append(beat)
            quantize(z_w[:], z_s[:], z_bf[beat][:])
            rows = y_f[beat // WIDE][:, :, beat % WIDE : beat % WIDE + width]
            side = WIDE // width
            for group, number in enumerate(numbers):
                acc = bank(f"y_acc{beat}_{group}", number)
                for u in range(side):
                    i = side * group + u
                    nc.tensor.matmul_mx(
                        out=acc[:, width * u : width * (u + 1)],
                        lhsT=wo_w[:, P * i : P * (i + 1)].bitcast(FP8X4),
                        lhsT_scale=wo_s[:, P * i : P * (i + 1)],
                        rhs=z_w[:].bitcast(FP8X4),
                        rhs_scale=z_s[:],
                        start=True, stop=True,
                    )
                nc.scalar.copy(rows[:, side * group : side * (group + 1), :], acc[:].rearrange("p (u t) -> p u t", u=side))
            nc.sync.dma_start(out_rows[:, :, beat : beat + width], rows)

        y_bf = {}

        def y_rows(start, width):
            return y_f[start // WIDE][:, :, start % WIDE : start % WIDE + width]

        def round_y(engine_copy, start, width, kb):
            y_bf[start] = new(f"y_bf{start}", [P, 4 * width], BF16, kb)
            weave(engine_copy, y_bf[start][:], y_rows(start, width), 2)

        def round_y_aside(start, width, kb):
            y_bf[start] = new(f"y_bf{start}", [P, 4 * width], BF16, kb)
            nc.gpsimd.tensor_scalar(
                y_bf[start][:].rearrange("p (t i) -> p t i", i=4), y_rows(start, width).rearrange("p i t -> p t i"),
                1.0, 0.0, MULT, ADD,
            )

        stores = {512: 0, 1024: 512, 1536: 1024, 1792: 1536, 2048: 1792}

        def planes_y(start, width):
            cols = slice(start, start + width)
            quantize(y_w[:, cols], y_s[:, cols], y_bf[start][:])
            if start + width in stores:
                cols = slice(stores[start + width], start + width)
                nc.sync.dma_start(out_words[:, cols], y_w[:, cols])

        make_z(0, P, 215)
        make_z(128, P, 216)
        make_y(0, P, [2])
        make_z(256, CHUNK, 217)
        make_y(128, P, [3])
        make_z(512, CHUNK, 219)
        make_y(256, CHUNK, [2, 3])
        make_y(512, CHUNK, [4, 5])
        round_y_aside(0, CHUNK, 219)
        make_z(768, CHUNK, 221)
        make_z(1024, CHUNK, 223)
        make_y(768, CHUNK, [6, 7])
        held[12] = turn_back(12, 2)
        held[13] = turn_back(13, 3)
        make_y(1024, CHUNK, [0, 1])
        round_y_aside(256, CHUNK, 223)
        held[14] = turn_back(14, 4)
        held[15] = turn_back(15, 5)
        make_z(1280, CHUNK, 157)
        make_z(1536, CHUNK, 124)
        y_w = new("y_w", [P, T2], I32, 157)
        make_y(1280, CHUNK, [6, 7])
        round_y(nc.scalar.copy, 768, CHUNK, 128)
        planes_y(0, CHUNK)
        planes_y(256, CHUNK)
        make_y(1536, CHUNK, [2, 3])
        round_y_aside(512, P, 223)
        round_y(nc.scalar.copy, 640, P, 126)
        make_z(1792, CHUNK, 133)
        make_y(1792, CHUNK, [4, 5])
        round_y(nc.scalar.copy, 1536, CHUNK, 136)
        round_y(nc.vector.tensor_copy, 1024, WIDE, 130)
        planes_y(512, P)
        planes_y(640, P)
        planes_y(768, CHUNK)
        planes_y(1024, WIDE)
        round_y(nc.vector.tensor_copy, 1792, CHUNK, 138)
        planes_y(1536, CHUNK)
        planes_y(1792, CHUNK)
        for q in range(4):
            nc.sync.dma_start(out_2[0, 4 * q : 4 * q + 4, :].bitcast(I32), y_s[32 * q : 32 * q + 4, :].bitcast(I32))
